import numpy as np
import ml_dtypes


def mxq(x, axis, fmt="e4m3"):
    dtype, down = {"e4m3": (ml_dtypes.float8_e4m3fn, 7), "e5m2": (ml_dtypes.float8_e5m2, 14)}[fmt]
    v = np.moveaxis(np.asarray(x, np.float32).astype(ml_dtypes.bfloat16).astype(np.float64), axis, -1)
    blocks = v.reshape(v.shape[:-1] + (-1, 32))
    amax = np.abs(blocks).max(-1, keepdims=True)
    byte = np.maximum(np.where(amax > 0, np.frexp(amax)[1] - 1 + 127, 0) - down, 1)
    scale = np.exp2(byte - 127.0)
    codes = (blocks / scale).astype(np.float32).astype(dtype).astype(np.float64)
    return np.moveaxis((codes * scale).reshape(v.shape), -1, axis)


WIDE = False


def mx_kscale(k):
    if not WIDE:
        return np.ones(k)
    levels = np.array([10, -10, 5, -5, 0])
    if k % 512:
        return np.exp2(np.random.permutation(np.resize(levels, k // 32))).repeat(32)
    a = np.empty((k // 512, 16))
    for p in range(k // 512):
        a[p, :8] = np.random.permutation(np.resize(levels, 8))
        for g in range(8):
            far = levels[np.abs(levels - a[p, g]) >= 10]
            a[p, g + 8] = far[np.random.randint(len(far))]
    return np.exp2(a.ravel()).repeat(32)


def f64(x):
    return np.asarray(x).astype(np.float64)


def striped(idx):
    return np.tile(idx.reshape(-1, 16).T, (8, 1)).astype(np.uint16)


def unstriped(offs):
    return offs[:16].T.reshape(-1).astype(np.int64)


def pack_weight(w):
    k, n = w.shape
    w = f64(np.asarray(w, np.float32).astype(ml_dtypes.bfloat16)).reshape(k // 32, 32, n)
    amax = np.abs(w).max(1)
    byte = np.clip(np.where(amax > 0, np.frexp(amax)[1] - 1 + 127 - 7, 1), 1, 254)
    scaled = (w * np.exp2(127.0 - byte)[:, None, :]).reshape(k, n).astype(np.float32)
    words = np.ascontiguousarray(scaled.reshape(k // 512, 128, 4, n).transpose(0, 1, 3, 2)).astype(ml_dtypes.float8_e4m3fn).view(np.uint8)
    return words, np.ascontiguousarray(byte.astype(np.uint8).reshape(k // 512, 16, n))


def unpack_weight(words, scales):
    g, p, n, _ = words.shape
    vals = np.ascontiguousarray(words).view(ml_dtypes.float8_e4m3fn).astype(np.float64) * np.repeat(np.exp2(scales.astype(np.float64) - 127.0), 8, axis=1)[..., None]
    return vals.transpose(0, 1, 3, 2).reshape(g * 512, n)


def relu(v):
    return np.maximum(v, 0.0)


K, T, S, V, H = 512, 1024, 512, 512, 512


def setup_inputs():
    n = np.random.standard_normal
    s = mx_kscale(K)[:, None]
    u = mx_kscale(H)
    packed_xT = pack_weight(n((K, T)) * s)
    return {
        "x_words": packed_xT[0],
        "x_scales": packed_xT[1],
        "w1": (n((K, H)) / np.sqrt(K) / s * u).astype(np.float32),
        "w2": (n((K, H)) / np.sqrt(K) / s / u / np.sqrt(H)).astype(np.float32),
        "offs": striped(np.random.permutation(T)[:S]),
        "dst": striped(np.random.permutation(T)[:V]),
    }


def reference(x_words, x_scales, w1, w2, offs, dst):
    xq = unpack_weight(x_words, x_scales)[:, unstriped(offs)]
    p = relu(mxq(f64(w1), 0, "e4m3").T @ xq)
    x_dst = unpack_weight(x_words, x_scales)[:, unstriped(dst)]
    d = relu(mxq(f64(w2), 0, "e4m3").T @ x_dst)
    y = mxq(p, 0, "e4m3").T @ mxq(d, 0, "e4m3")
    e = np.exp(y - y.max(axis=1, keepdims=True))
    return e / e.sum(axis=1, keepdims=True)

@@ -1,0 +1,153 @@
+from contextlib import ExitStack
+
+import concourse.mybir as mybir
+
+K, T, S, V, H = 512, 1024, 512, 512, 512
+FLOPS = 2 * K * H * S + 2 * K * H * V + 2 * H * S * V
+
+F32 = mybir.dt.float32
+BF16 = mybir.dt.bfloat16
+I32 = mybir.dt.int32
+U32 = mybir.dt.uint32
+U16 = mybir.dt.uint16
+U8 = mybir.dt.uint8
+FP8X4 = mybir.dt.float8_e4m3fn_x4
+ACT = mybir.ActivationFunctionType
+ALU = mybir.AluOpType
+
+P = 128
+PACK = 4
+CHUNK = 128
+CHUNKS = 4
+HALF = 256
+
+
+def tile_picked_zlink_reluxsoft_p_kernel(tc, x_words, x_scales, w1, w2, offs, dst, out):
+    nc = tc.nc
+    with ExitStack() as ctx:
+        keep = ctx.enter_context(tc.tile_pool(name="keep", bufs=1))
+        hid_psum = ctx.enter_context(tc.psum_pool(name="hid_psum", bufs=5))
+        score_psum = ctx.enter_context(tc.psum_pool(name="score_psum", bufs=3))
+
+        dst_list = keep.tile([P, V // 16], U16, name="dst_list")
+        src_list = keep.tile([P, S // 16], U16, name="src_list")
+        scale_table = keep.tile([P, T], U8, name="scale_table", align_bytes=64)
+        word_table = keep.tile([P, T], I32, name="word_table", align_bytes=64)
+
+        warm_in = keep.tile([P, 1], F32, name="warm_in")
+        warm_out = keep.tile([P, 1], F32, name="warm_out")
+        nc.vector.memset(scale_table[:].bitcast(I32), 0)
+        nc.gpsimd.memset(warm_in[:], 0.0)
+        nc.scalar.activation(warm_out[:], warm_in[:], ACT.Exp)
+
+        nc.sync.dma_start(dst_list[:], dst)
+        nc.sync.dma_start(src_list[:], offs)
+        for q in range(4):
+            nc.sync.dma_start(scale_table[32 * q : 32 * q + 4, :].bitcast(I32), x_scales[0, 4 * q : 4 * q + 4, :].bitcast(I32))
+        nc.sync.dma_start(word_table[:], x_words[0].rearrange("p c r -> p (c r)").bitcast(I32))
+
+        raw = {}
+        for name, w in (("w2", w2), ("w1", w1)):
+            for h in range(2):
+                raw[name, h] = keep.tile([P, PACK, HALF], F32, name=f"raw_{name}_{h}", align_bytes=64)
+                nc.sync.dma_start(raw[name, h][:], w.rearrange("(p j) c -> p j c", j=PACK)[:, :, h * HALF : (h + 1) * HALF])
+
+        def picked(name):
+            words = [keep.tile([P, CHUNK], U32, name=f"{name}_words{c}", align_bytes=64) for c in range(CHUNKS)]
+            scales = keep.tile([P, CHUNKS * CHUNK], U8, name=f"{name}_scales", align_bytes=64)
+            return words, scales
+
+        xd_words, xd_scales = picked("xd")
+        xs_words, xs_scales = picked("xs")
+
+        def gather_scales(scales, offsets):
+            nc.vector.tensor_copy(scales[:], scale_table[:].indirect(offsets[:]))
+
+        def gather_words(words, offsets):
+            for c in range(CHUNKS):
+                nc.vector.tensor_copy(words[c][:], word_table[:].bitcast(U32).indirect(offsets[:, 8 * c : 8 * c + 8]))
+
+        grouped = {n: keep.tile([P, H * PACK], BF16, name=f"grouped_{n}", align_bytes=64) for n in ("w1", "w2")}
+        w_words = {n: keep.tile([P, H], U32, name=f"words_{n}", align_bytes=64) for n in ("w1", "w2")}
+        w_scales = {n: keep.tile([P, H], U8, name=f"scales_{n}", align_bytes=64) for n in ("w1", "w2")}
+
+        def round_weights(name, h, copy):
+            dest = grouped[name][:].rearrange("p (t g i j) -> p t g j i", t=4, i=4, j=PACK)[:, :, 16 * h : 16 * h + 16]
+            copy(dest, raw[name, h][:].rearrange("p j (g t i) -> p t g j i", t=4, i=4))
+
+        def quantize_weights(name):
+            nc.vector.quantize_mx(out=w_words[name][:].bitcast(FP8X4), scales=w_scales[name][:], in_=grouped[name][:])
+
+        def hidden_matmuls(name, words, scales, c):
+            bank = hid_psum.tile([P, PACK, CHUNK], F32, name="hid_bank")
+            for t in range(PACK):
+                cols = slice(t * P, (t + 1) * P)
+                nc.tensor.matmul_mx(
+                    out=bank[:, t, :],
+                    lhsT=w_words[name][:, cols].bitcast(FP8X4),
+                    lhsT_scale=w_scales[name][:, cols],
+                    rhs=words[c][:].bitcast(FP8X4),
+                    rhs_scale=scales[:, c * CHUNK : (c + 1) * CHUNK],
+                    start=True,
+                    stop=True,
+                )
+            return bank
+
+        def relu(name, bank, on_scalar):
+            hidden = keep.tile([P, CHUNK * PACK], BF16, name=name, align_bytes=64)
+            dest = hidden[:].rearrange("p (n t) -> p n t", t=PACK)
+            source = bank[:].rearrange("p t n -> p n t")
+            if on_scalar:
+                nc.scalar.activation(dest, source, ACT.Relu)
+            else:
+                nc.vector.tensor_scalar(dest, source, 0.0, None, ALU.max)
+            return hidden
+
+        gather_scales(xd_scales, dst_list)
+        gather_words(xd_words, dst_list)
+        gather_scales(xs_scales, src_list)
+        gather_words(xs_words, src_list)
+        round_weights("w2", 0, nc.scalar.copy)
+        round_weights("w2", 1, nc.scalar.copy)
+        round_weights("w1", 0, nc.scalar.copy)
+        quantize_weights("w2")
+        d_banks = [hidden_matmuls("w2", xd_words, xd_scales, c) for c in range(CHUNKS)]
+        round_weights("w1", 1, nc.vector.tensor_copy)
+        quantize_weights("w1")
+
+        d_words = keep.tile([P, V], U32, name="d_words", align_bytes=64)
+        d_scales = keep.tile([P, V], U8, name="d_scales", align_bytes=64)
+        for c in range(CHUNKS):
+            hidden = relu(f"d_hidden{c}", d_banks[c], True)
+            cols = slice(c * CHUNK, (c + 1) * CHUNK)
+            nc.vector.quantize_mx(out=d_words[:, cols].bitcast(FP8X4), scales=d_scales[:, cols], in_=hidden[:])
+
+        p_words, p_scales = [], []
+        for c in range(CHUNKS):
+            bank = hidden_matmuls("w1", xs_words, xs_scales, c)
+            hidden = relu(f"p_hidden{c}", bank, c % 2 == 1)
+            p_words.append(keep.tile([P, CHUNK], U32, name=f"p_words{c}", align_bytes=64))
+            p_scales.append(keep.tile([P, CHUNK], U8, name=f"p_scales{c}", align_bytes=64))
+            nc.vector.quantize_mx(out=p_words[c][:].bitcast(FP8X4), scales=p_scales[c][:], in_=hidden[:])
+
+        for c in range(CHUNKS):
+            score = score_psum.tile([P, V], F32, name="score")
+            nc.tensor.matmul_mx(
+                out=score[:],
+                lhsT=p_words[c][:].bitcast(FP8X4),
+                lhsT_scale=p_scales[c][:],
+                rhs=d_words[:].bitcast(FP8X4),
+                rhs_scale=d_scales[:],
+                start=True,
+                stop=True,
+            )
+            neg_max = keep.tile([P, 1], F32, name=f"neg_max{c}")
+            total = keep.tile([P, 1], F32, name=f"total{c}")
+            inverse = keep.tile([P, 1], F32, name=f"inverse{c}")
+            powers = keep.tile([P, V], F32, name=f"powers{c}")
+            result = keep.tile([P, V], F32, name=f"result{c}")
+            nc.vector.tensor_reduce(neg_max[:], score[:], mybir.AxisListType.X, ALU.max, negate=True)
+            nc.scalar.activation(powers[:], score[:], ACT.Exp, bias=neg_max[:], accum_out=total[:])
+            nc.vector.reciprocal(inverse[:], total[:])
+            nc.vector.tensor_scalar(result[:], powers[:], inverse[:], None, ALU.mult)
+            nc.sync.dma_start(out[c * CHUNK : (c + 1) * CHUNK, :], result[:])

@@ -26,8 +26,7 @@ def tile_picked_zlink_reluxsoft_p_kernel(tc, x_words, x_scales, w1, w2, offs, ds
     nc = tc.nc
     with ExitStack() as ctx:
         keep = ctx.enter_context(tc.tile_pool(name="keep", bufs=1))
-        hid_psum = ctx.enter_context(tc.psum_pool(name="hid_psum", bufs=5))
-        score_psum = ctx.enter_context(tc.psum_pool(name="score_psum", bufs=3))
+        psum = ctx.enter_context(tc.psum_pool(name="psum", bufs=8))
 
         dst_list = keep.tile([P, V // 16], U16, name="dst_list")
         src_list = keep.tile([P, S // 16], U16, name="src_list")
@@ -37,13 +36,12 @@ def tile_picked_zlink_reluxsoft_p_kernel(tc, x_words, x_scales, w1, w2, offs, ds
         warm_in = keep.tile([P, 1], F32, name="warm_in")
         warm_out = keep.tile([P, 1], F32, name="warm_out")
         nc.vector.memset(scale_table[:].bitcast(I32), 0)
-        nc.gpsimd.memset(warm_in[:], 0.0)
-        nc.scalar.activation(warm_out[:], warm_in[:], ACT.Exp)
+        nc.vector.memset(warm_in[:], 0.0)
 
         nc.sync.dma_start(dst_list[:], dst)
-        nc.sync.dma_start(src_list[:], offs)
         for q in range(4):
-            nc.sync.dma_start(scale_table[32 * q : 32 * q + 4, :].bitcast(I32), x_scales[0, 4 * q : 4 * q + 4, :].bitcast(I32))
+            nc.scalar.dma_start(scale_table[32 * q : 32 * q + 4, :].bitcast(I32), x_scales[0, 4 * q : 4 * q + 4, :].bitcast(I32))
+        nc.scalar.activation(warm_out[:], warm_in[:], ACT.Exp)
         nc.sync.dma_start(word_table[:], x_words[0].rearrange("p c r -> p (c r)").bitcast(I32))
 
         raw = {}
@@ -51,21 +49,18 @@ def tile_picked_zlink_reluxsoft_p_kernel(tc, x_words, x_scales, w1, w2, offs, ds
             for h in range(2):
                 raw[name, h] = keep.tile([P, PACK, HALF], F32, name=f"raw_{name}_{h}", align_bytes=64)
                 nc.sync.dma_start(raw[name, h][:], w.rearrange("(p j) c -> p j c", j=PACK)[:, :, h * HALF : (h + 1) * HALF])
+                if (name, h) == ("w2", 0):
+                    nc.sync.dma_start(src_list[:], offs)
 
-        def picked(name):
-            words = [keep.tile([P, CHUNK], U32, name=f"{name}_words{c}", align_bytes=64) for c in range(CHUNKS)]
-            scales = keep.tile([P, CHUNKS * CHUNK], U8, name=f"{name}_scales", align_bytes=64)
-            return words, scales
-
-        xd_words, xd_scales = picked("xd")
-        xs_words, xs_scales = picked("xs")
-
-        def gather_scales(scales, offsets):
+        def gather_scales(name, offsets):
+            scales = keep.tile([P, CHUNKS * CHUNK], U8, name=name, align_bytes=64)
             nc.vector.tensor_copy(scales[:], scale_table[:].indirect(offsets[:]))
+            return scales
 
-        def gather_words(words, offsets):
-            for c in range(CHUNKS):
-                nc.vector.tensor_copy(words[c][:], word_table[:].bitcast(U32).indirect(offsets[:, 8 * c : 8 * c + 8]))
+        def gather_words(name, offsets, tag):
+            words = keep.tile([P, 16 * offsets.shape[1]], U32, name=name, tag=tag, align_bytes=64)
+            nc.vector.tensor_copy(words[:], word_table[:].bitcast(U32).indirect(offsets))
+            return words
 
         grouped = {n: keep.tile([P, H * PACK], BF16, name=f"grouped_{n}", align_bytes=64) for n in ("w1", "w2")}
         w_words = {n: keep.tile([P, H], U32, name=f"words_{n}", align_bytes=64) for n in ("w1", "w2")}
@@ -78,60 +73,60 @@ def tile_picked_zlink_reluxsoft_p_kernel(tc, x_words, x_scales, w1, w2, offs, ds
         def quantize_weights(name):
             nc.vector.quantize_mx(out=w_words[name][:].bitcast(FP8X4), scales=w_scales[name][:], in_=grouped[name][:])
 
-        def hidden_matmuls(name, words, scales, c):
-            bank = hid_psum.tile([P, PACK, CHUNK], F32, name="hid_bank")
+        def hidden_matmuls(name, words, scales):
+            bank = psum.tile([P, PACK, CHUNK], F32, name="hid_bank", tag="bank")
             for t in range(PACK):
                 cols = slice(t * P, (t + 1) * P)
                 nc.tensor.matmul_mx(
                     out=bank[:, t, :],
                     lhsT=w_words[name][:, cols].bitcast(FP8X4),
                     lhsT_scale=w_scales[name][:, cols],
-                    rhs=words[c][:].bitcast(FP8X4),
-                    rhs_scale=scales[:, c * CHUNK : (c + 1) * CHUNK],
+                    rhs=words.bitcast(FP8X4),
+                    rhs_scale=scales,
                     start=True,
                     stop=True,
                 )
             return bank
 
-        def relu(name, bank, on_scalar):
-            hidden = keep.tile([P, CHUNK * PACK], BF16, name=name, align_bytes=64)
-            dest = hidden[:].rearrange("p (n t) -> p n t", t=PACK)
-            source = bank[:].rearrange("p t n -> p n t")
-            if on_scalar:
-                nc.scalar.activation(dest, source, ACT.Relu)
-            else:
-                nc.vector.tensor_scalar(dest, source, 0.0, None, ALU.max)
-            return hidden
+        def relu(hidden, bank):
+            nc.scalar.activation(hidden.rearrange("p (n t) -> p n t", t=PACK), bank[:].rearrange("p t n -> p n t"), ACT.Relu)
 
-        gather_scales(xd_scales, dst_list)
-        gather_words(xd_words, dst_list)
-        gather_scales(xs_scales, src_list)
-        gather_words(xs_words, src_list)
+        def chunk(tile, c):
+            return tile[:, c * CHUNK : (c + 1) * CHUNK]
+
+        xd_scales = gather_scales("xd_scales", dst_list)
+        xd_words = gather_words("xd_words", dst_list[:], "xd_words")
         round_weights("w2", 0, nc.scalar.copy)
         round_weights("w2", 1, nc.scalar.copy)
+        xs_scales = gather_scales("xs_scales", src_list)
         round_weights("w1", 0, nc.scalar.copy)
         quantize_weights("w2")
-        d_banks = [hidden_matmuls("w2", xd_words, xd_scales, c) for c in range(CHUNKS)]
+        xs_words = [gather_words("xs_words0", src_list[:, 0:16], "raw_w2_1")]
+        d_banks = [hidden_matmuls("w2", chunk(xd_words, c), chunk(xd_scales, c)) for c in range(CHUNKS)]
         round_weights("w1", 1, nc.vector.tensor_copy)
         quantize_weights("w1")
+        xs_words.append(gather_words("xs_words1", src_list[:, 16:32], "grouped_w1"))
 
         d_words = keep.tile([P, V], U32, name="d_words", align_bytes=64)
         d_scales = keep.tile([P, V], U8, name="d_scales", align_bytes=64)
-        for c in range(CHUNKS):
-            hidden = relu(f"d_hidden{c}", d_banks[c], True)
-            cols = slice(c * CHUNK, (c + 1) * CHUNK)
+        for h in range(2):
+            hidden = keep.tile([P, HALF * PACK], BF16, name=f"d_hidden{h}", align_bytes=64)
+            for c in range(2):
+                relu(hidden[:, c * CHUNK * PACK : (c + 1) * CHUNK * PACK], d_banks[2 * h + c])
+            cols = slice(h * HALF, (h + 1) * HALF)
             nc.vector.quantize_mx(out=d_words[:, cols].bitcast(FP8X4), scales=d_scales[:, cols], in_=hidden[:])
 
         p_words, p_scales = [], []
         for c in range(CHUNKS):
-            bank = hidden_matmuls("w1", xs_words, xs_scales, c)
-            hidden = relu(f"p_hidden{c}", bank, c % 2 == 1)
+            bank = hidden_matmuls("w1", chunk(xs_words[c // 2], c % 2), chunk(xs_scales, c))
+            hidden = keep.tile([P, CHUNK * PACK], BF16, name=f"p_hidden{c}", align_bytes=64)
+            relu(hidden[:], bank)
             p_words.append(keep.tile([P, CHUNK], U32, name=f"p_words{c}", align_bytes=64))
             p_scales.append(keep.tile([P, CHUNK], U8, name=f"p_scales{c}", align_bytes=64))
             nc.vector.quantize_mx(out=p_words[c][:].bitcast(FP8X4), scales=p_scales[c][:], in_=hidden[:])
 
         for c in range(CHUNKS):
-            score = score_psum.tile([P, V], F32, name="score")
+            score = psum.tile([P, V], F32, name="score", tag="bank")
             nc.tensor.matmul_mx(
                 out=score[:],
                 lhsT=p_words[c][:].bitcast(FP8X4),
@@ -149,5 +144,8 @@ def tile_picked_zlink_reluxsoft_p_kernel(tc, x_words, x_scales, w1, w2, offs, ds
             nc.vector.tensor_reduce(neg_max[:], score[:], mybir.AxisListType.X, ALU.max, negate=True)
             nc.scalar.activation(powers[:], score[:], ACT.Exp, bias=neg_max[:], accum_out=total[:])
             nc.vector.reciprocal(inverse[:], total[:])
-            nc.vector.tensor_scalar(result[:], powers[:], inverse[:], None, ALU.mult)
+            if c < 1:
+                nc.gpsimd.tensor_scalar(result[:], powers[:], inverse[:], 0.0, ALU.mult, ALU.add)
+            else:
+                nc.vector.tensor_scalar(result[:], powers[:], inverse[:], None, ALU.mult)
             nc.sync.dma_start(out[c * CHUNK : (c + 1) * CHUNK, :], result[:])

@@ -33,15 +33,11 @@ def tile_picked_zlink_reluxsoft_p_kernel(tc, x_words, x_scales, w1, w2, offs, ds
         scale_table = keep.tile([P, T], U8, name="scale_table", align_bytes=64)
         word_table = keep.tile([P, T], I32, name="word_table", align_bytes=64)
 
-        warm_in = keep.tile([P, 1], F32, name="warm_in")
-        warm_out = keep.tile([P, 1], F32, name="warm_out")
         nc.vector.memset(scale_table[:].bitcast(I32), 0)
-        nc.vector.memset(warm_in[:], 0.0)
 
         nc.sync.dma_start(dst_list[:], dst)
         for q in range(4):
             nc.scalar.dma_start(scale_table[32 * q : 32 * q + 4, :].bitcast(I32), x_scales[0, 4 * q : 4 * q + 4, :].bitcast(I32))
-        nc.scalar.activation(warm_out[:], warm_in[:], ACT.Exp)
         nc.sync.dma_start(word_table[:], x_words[0].rearrange("p c r -> p (c r)").bitcast(I32))
 
         raw = {}

@@ -32,21 +32,17 @@ def tile_picked_zlink_reluxsoft_p_kernel(tc, x_words, x_scales, w1, w2, offs, ds
         src_list = keep.tile([P, S // 16], U16, name="src_list")
         scale_table = keep.tile([P, T], U8, name="scale_table", align_bytes=64)
         word_table = keep.tile([P, T], I32, name="word_table", align_bytes=64)
+        raw = {(n, h): keep.tile([P, PACK, HALF], F32, name=f"raw_{n}_{h}", align_bytes=64) for n in ("w1", "w2") for h in range(2)}
+        weights = {"w1": w1, "w2": w2}
 
-        nc.vector.memset(scale_table[:].bitcast(I32), 0)
+        def load_scales(q, queue):
+            queue.dma_start(scale_table[32 * q : 32 * q + 4, :].bitcast(I32), x_scales[0, 4 * q : 4 * q + 4, :].bitcast(I32))
 
-        nc.sync.dma_start(dst_list[:], dst)
-        for q in range(4):
-            nc.scalar.dma_start(scale_table[32 * q : 32 * q + 4, :].bitcast(I32), x_scales[0, 4 * q : 4 * q + 4, :].bitcast(I32))
-        nc.sync.dma_start(word_table[:], x_words[0].rearrange("p c r -> p (c r)").bitcast(I32))
+        def load_words(queue):
+            queue.dma_start(word_table[:], x_words[0].rearrange("p c r -> p (c r)").bitcast(I32))
 
-        raw = {}
-        for name, w in (("w2", w2), ("w1", w1)):
-            for h in range(2):
-                raw[name, h] = keep.tile([P, PACK, HALF], F32, name=f"raw_{name}_{h}", align_bytes=64)
-                nc.sync.dma_start(raw[name, h][:], w.rearrange("(p j) c -> p j c", j=PACK)[:, :, h * HALF : (h + 1) * HALF])
-                if (name, h) == ("w2", 0):
-                    nc.sync.dma_start(src_list[:], offs)
+        def load_weights(name, h, queue):
+            queue.dma_start(raw[name, h][:], weights[name].rearrange("(p j) c -> p j c", j=PACK)[:, :, h * HALF : (h + 1) * HALF])
 
         def gather_scales(name, offsets):
             scales = keep.tile([P, CHUNKS * CHUNK], U8, name=name, align_bytes=64)
@@ -62,9 +58,13 @@ def tile_picked_zlink_reluxsoft_p_kernel(tc, x_words, x_scales, w1, w2, offs, ds
         w_words = {n: keep.tile([P, H], U32, name=f"words_{n}", align_bytes=64) for n in ("w1", "w2")}
         w_scales = {n: keep.tile([P, H], U8, name=f"scales_{n}", align_bytes=64) for n in ("w1", "w2")}
 
-        def round_weights(name, h, copy):
-            dest = grouped[name][:].rearrange("p (t g i j) -> p t g j i", t=4, i=4, j=PACK)[:, :, 16 * h : 16 * h + 16]
-            copy(dest, raw[name, h][:].rearrange("p j (g t i) -> p t g j i", t=4, i=4))
+        def round_weights(name, h, copy, t0=0, t1=PACK):
+            dest = grouped[name][:].rearrange("p (t g i j) -> p t g j i", t=4, i=4, j=PACK)[:, t0:t1, 16 * h : 16 * h + 16]
+            copy(dest, raw[name, h][:].rearrange("p j (g t i) -> p t g j i", t=4, i=4)[:, t0:t1])
+
+        def round_weights_gpsimd(name, h, t0, t1):
+            dest = grouped[name][:].rearrange("p (t g i j) -> p g t i j", t=4, i=4, j=PACK)[:, 16 * h : 16 * h + 16, t0:t1]
+            nc.gpsimd.tensor_scalar(dest, raw[name, h][:].rearrange("p j (g t i) -> p g t i j", t=4, i=4)[:, :, t0:t1], 1.0, 0.0, ALU.mult, ALU.add)
 
         def quantize_weights(name):
             nc.vector.quantize_mx(out=w_words[name][:].bitcast(FP8X4), scales=w_scales[name][:], in_=grouped[name][:])
@@ -87,41 +87,36 @@ def tile_picked_zlink_reluxsoft_p_kernel(tc, x_words, x_scales, w1, w2, offs, ds
         def relu(hidden, bank):
             nc.scalar.activation(hidden.rearrange("p (n t) -> p n t", t=PACK), bank[:].rearrange("p t n -> p n t"), ACT.Relu)
 
+        def relu_vector(hidden, bank):
+            nc.vector.tensor_scalar(hidden.rearrange("p (n t) -> p n t", t=PACK), bank[:].rearrange("p t n -> p n t"), 0.0, None, ALU.max)
+
         def chunk(tile, c):
             return tile[:, c * CHUNK : (c + 1) * CHUNK]
 
-        xd_scales = gather_scales("xd_scales", dst_list)
-        xd_words = gather_words("xd_words", dst_list[:], "xd_words")
-        round_weights("w2", 0, nc.scalar.copy)
-        round_weights("w2", 1, nc.scalar.copy)
-        xs_scales = gather_scales("xs_scales", src_list)
-        round_weights("w1", 0, nc.scalar.copy)
-        quantize_weights("w2")
-        xs_words = [gather_words("xs_words0", src_list[:, 0:16], "raw_w2_1")]
-        d_banks = [hidden_matmuls("w2", chunk(xd_words, c), chunk(xd_scales, c)) for c in range(CHUNKS)]
-        round_weights("w1", 1, nc.vector.tensor_copy)
-        quantize_weights("w1")
-        xs_words.append(gather_words("xs_words1", src_list[:, 16:32], "grouped_w1"))
-
         d_words = keep.tile([P, V], U32, name="d_words", align_bytes=64)
         d_scales = keep.tile([P, V], U8, name="d_scales", align_bytes=64)
-        for h in range(2):
-            hidden = keep.tile([P, HALF * PACK], BF16, name=f"d_hidden{h}", align_bytes=64)
-            for c in range(2):
-                relu(hidden[:, c * CHUNK * PACK : (c + 1) * CHUNK * PACK], d_banks[2 * h + c])
+        d_hidden = [keep.tile([P, HALF * PACK], BF16, name=f"d_hidden{h}", align_bytes=64) for h in range(2)]
+        p_hidden = [keep.tile([P, CHUNK * PACK], BF16, name=f"p_hidden{c}", align_bytes=64) for c in range(CHUNKS)]
+        p_words = [keep.tile([P, CHUNK], U32, name=f"p_words{c}", align_bytes=64) for c in range(CHUNKS)]
+        p_scales = [keep.tile([P, CHUNK], U8, name=f"p_scales{c}", align_bytes=64) for c in range(CHUNKS)]
+
+        def d_part(c):
+            return d_hidden[c // 2][:, (c % 2) * CHUNK * PACK : (c % 2 + 1) * CHUNK * PACK]
+
+        def quantize_d(h):
             cols = slice(h * HALF, (h + 1) * HALF)
-            nc.vector.quantize_mx(out=d_words[:, cols].bitcast(FP8X4), scales=d_scales[:, cols], in_=hidden[:])
+            nc.vector.quantize_mx(out=d_words[:, cols].bitcast(FP8X4), scales=d_scales[:, cols], in_=d_hidden[h][:])
 
-        p_words, p_scales = [], []
-        for c in range(CHUNKS):
-            bank = hidden_matmuls("w1", chunk(xs_words[c // 2], c % 2), chunk(xs_scales, c))
-            hidden = keep.tile([P, CHUNK * PACK], BF16, name=f"p_hidden{c}", align_bytes=64)
-            relu(hidden[:], bank)
-            p_words.append(keep.tile([P, CHUNK], U32, name=f"p_words{c}", align_bytes=64))
-            p_scales.append(keep.tile([P, CHUNK], U8, name=f"p_scales{c}", align_bytes=64))
-            nc.vector.quantize_mx(out=p_words[c][:].bitcast(FP8X4), scales=p_scales[c][:], in_=hidden[:])
+        def quantize_p(c):
+            nc.vector.quantize_mx(out=p_words[c][:].bitcast(FP8X4), scales=p_scales[c][:], in_=p_hidden[c][:])
 
-        for c in range(CHUNKS):
+        neg_max = [keep.tile([P, 1], F32, name=f"neg_max{c}") for c in range(CHUNKS)]
+        total = [keep.tile([P, 1], F32, name=f"total{c}") for c in range(CHUNKS)]
+        inverse = [keep.tile([P, 1], F32, name=f"inverse{c}") for c in range(CHUNKS)]
+        powers = [keep.tile([P, V], F32, name=f"powers{c}") for c in range(CHUNKS)]
+        result = [keep.tile([P, V], F32, name=f"result{c}") for c in range(CHUNKS)]
+
+        def score_matmul(c):
             score = psum.tile([P, V], F32, name="score", tag="bank")
             nc.tensor.matmul_mx(
                 out=score[:],
@@ -132,16 +127,67 @@ def tile_picked_zlink_reluxsoft_p_kernel(tc, x_words, x_scales, w1, w2, offs, ds
                 start=True,
                 stop=True,
             )
-            neg_max = keep.tile([P, 1], F32, name=f"neg_max{c}")
-            total = keep.tile([P, 1], F32, name=f"total{c}")
-            inverse = keep.tile([P, 1], F32, name=f"inverse{c}")
-            powers = keep.tile([P, V], F32, name=f"powers{c}")
-            result = keep.tile([P, V], F32, name=f"result{c}")
-            nc.vector.tensor_reduce(neg_max[:], score[:], mybir.AxisListType.X, ALU.max, negate=True)
-            nc.scalar.activation(powers[:], score[:], ACT.Exp, bias=neg_max[:], accum_out=total[:])
-            nc.vector.reciprocal(inverse[:], total[:])
-            if c < 1:
-                nc.gpsimd.tensor_scalar(result[:], powers[:], inverse[:], 0.0, ALU.mult, ALU.add)
+            return score
+
+        def row_max(c, score):
+            nc.vector.tensor_reduce(neg_max[c][:], score[:], mybir.AxisListType.X, ALU.max, negate=True)
+
+        def exponentials(c, score):
+            nc.scalar.activation(powers[c][:], score[:], ACT.Exp, bias=neg_max[c][:], accum_out=total[c][:])
+
+        def invert(c):
+            nc.vector.reciprocal(inverse[c][:], total[c][:])
+
+        def normalise_gpsimd(c):
+            nc.gpsimd.tensor_scalar(result[c][:], powers[c][:], inverse[c][:], 0.0, ALU.mult, ALU.add)
+
+        def normalise_vector(c):
+            nc.vector.tensor_scalar(result[c][:], powers[c][:], inverse[c][:], None, ALU.mult)
+
+        def store(c):
+            nc.sync.dma_start(out[c * CHUNK : (c + 1) * CHUNK, :], result[c][:])
+
+        nc.vector.memset(scale_table[:].bitcast(I32), 0)
+        nc.sync.dma_start(dst_list[:], dst)
+        for q in range(4):
+            load_scales(q, nc.scalar)
+        load_words(nc.sync)
+        load_weights("w2", 0, nc.sync)
+        nc.sync.dma_start(src_list[:], offs)
+        load_weights("w2", 1, nc.sync)
+        load_weights("w1", 0, nc.sync)
+        load_weights("w1", 1, nc.sync)
+
+        xd_scales = gather_scales("xd_scales", dst_list)
+        xd_words = gather_words("xd_words", dst_list[:], "xd_words")
+        round_weights("w2", 0, nc.scalar.copy, 0, 3)
+        round_weights_gpsimd("w2", 0, 3, 4)
+        round_weights("w2", 1, nc.scalar.copy, 0, 3)
+        round_weights_gpsimd("w2", 1, 3, 4)
+        xs_scales = gather_scales("xs_scales", src_list)
+        round_weights("w1", 0, nc.scalar.copy, 0, 2)
+        round_weights_gpsimd("w1", 0, 2, 4)
+        quantize_weights("w2")
+        xs_words = [gather_words("xs_words0", src_list[:, 0:16], "raw_w2_1")]
+        d_banks = [hidden_matmuls("w2", chunk(xd_words, c), chunk(xd_scales, c)) for c in range(CHUNKS)]
+        round_weights("w1", 1, nc.vector.tensor_copy)
+        quantize_weights("w1")
+        xs_words.append(gather_words("xs_words1", src_list[:, 16:32], "grouped_w1"))
+        for c in range(CHUNKS):
+            relu(d_part(c), d_banks[c])
+            if c % 2 == 1:
+                quantize_d(c // 2)
+        for c in range(CHUNKS):
+            bank = hidden_matmuls("w1", chunk(xs_words[c // 2], c % 2), chunk(xs_scales, c))
+            relu(p_hidden[c][:], bank)
+            quantize_p(c)
+        for c in range(CHUNKS):
+            score = score_matmul(c)
+            row_max(c, score)
+            exponentials(c, score)
+            invert(c)
+            if c < 2:
+                normalise_gpsimd(c)
             else:
-                nc.vector.tensor_scalar(result[:], powers[:], inverse[:], None, ALU.mult)
-            nc.sync.dma_start(out[c * CHUNK : (c + 1) * CHUNK, :], result[:])
+                normalise_vector(c)
+            store(c)

@@ -26,13 +26,14 @@ def tile_picked_zlink_reluxsoft_p_kernel(tc, x_words, x_scales, w1, w2, offs, ds
     nc = tc.nc
     with ExitStack() as ctx:
         keep = ctx.enter_context(tc.tile_pool(name="keep", bufs=1))
+        shared = ctx.enter_context(tc.tile_pool(name="shared", bufs=1))
         psum = ctx.enter_context(tc.psum_pool(name="psum", bufs=8))
 
         dst_list = keep.tile([P, V // 16], U16, name="dst_list")
         src_list = keep.tile([P, S // 16], U16, name="src_list")
         scale_table = keep.tile([P, T], U8, name="scale_table", align_bytes=64)
         word_table = keep.tile([P, T], I32, name="word_table", align_bytes=64)
-        raw = {(n, h): keep.tile([P, PACK, HALF], F32, name=f"raw_{n}_{h}", align_bytes=64) for n in ("w1", "w2") for h in range(2)}
+        raw = {n: keep.tile([P, PACK, H], F32, name=f"raw_{n}", align_bytes=64) for n in ("w1", "w2")}
         weights = {"w1": w1, "w2": w2}
 
         def load_scales(q, queue):
@@ -41,30 +42,30 @@ def tile_picked_zlink_reluxsoft_p_kernel(tc, x_words, x_scales, w1, w2, offs, ds
         def load_words(queue):
             queue.dma_start(word_table[:], x_words[0].rearrange("p c r -> p (c r)").bitcast(I32))
 
-        def load_weights(name, h, queue):
-            queue.dma_start(raw[name, h][:], weights[name].rearrange("(p j) c -> p j c", j=PACK)[:, :, h * HALF : (h + 1) * HALF])
+        def load_weights(name, queue):
+            queue.dma_start(raw[name][:], weights[name].rearrange("(p j) c -> p j c", j=PACK))
 
-        def gather_scales(name, offsets):
-            scales = keep.tile([P, CHUNKS * CHUNK], U8, name=name, align_bytes=64)
-            nc.vector.tensor_copy(scales[:], scale_table[:].indirect(offsets[:]))
+        def gather_scales(name, offsets, at=None):
+            scales = (keep if at is None else shared).tile([P, 16 * offsets.shape[1]], U8, name=name, align_bytes=64, offset=at)
+            nc.vector.tensor_copy(scales[:], scale_table[:].indirect(offsets))
             return scales
 
-        def gather_words(name, offsets, tag):
-            words = keep.tile([P, 16 * offsets.shape[1]], U32, name=name, tag=tag, align_bytes=64)
+        def gather_words(name, offsets, at=None):
+            words = (keep if at is None else shared).tile([P, 16 * offsets.shape[1]], U32, name=name, align_bytes=64, offset=at)
             nc.vector.tensor_copy(words[:], word_table[:].bitcast(U32).indirect(offsets))
             return words
 
-        grouped = {n: keep.tile([P, H * PACK], BF16, name=f"grouped_{n}", align_bytes=64) for n in ("w1", "w2")}
+        grouped = {n: shared.tile([P, H * PACK], BF16, name=f"grouped_{n}", align_bytes=64, offset=at) for n, at in (("w2", 0), ("w1", 4096))}
         w_words = {n: keep.tile([P, H], U32, name=f"words_{n}", align_bytes=64) for n in ("w1", "w2")}
         w_scales = {n: keep.tile([P, H], U8, name=f"scales_{n}", align_bytes=64) for n in ("w1", "w2")}
 
-        def round_weights(name, h, copy, t0=0, t1=PACK):
-            dest = grouped[name][:].rearrange("p (t g i j) -> p t g j i", t=4, i=4, j=PACK)[:, t0:t1, 16 * h : 16 * h + 16]
-            copy(dest, raw[name, h][:].rearrange("p j (g t i) -> p t g j i", t=4, i=4)[:, t0:t1])
+        def round_weights(name, copy, t0, t1):
+            dest = grouped[name][:].rearrange("p (t g i j) -> p t g j i", t=4, i=4, j=PACK)[:, t0:t1]
+            copy(dest, raw[name][:].rearrange("p j (g t i) -> p t g j i", t=4, i=4)[:, t0:t1])
 
-        def round_weights_gpsimd(name, h, t0, t1):
-            dest = grouped[name][:].rearrange("p (t g i j) -> p g t i j", t=4, i=4, j=PACK)[:, 16 * h : 16 * h + 16, t0:t1]
-            nc.gpsimd.tensor_scalar(dest, raw[name, h][:].rearrange("p j (g t i) -> p g t i j", t=4, i=4)[:, :, t0:t1], 1.0, 0.0, ALU.mult, ALU.add)
+        def round_weights_gpsimd(name, t0, t1):
+            dest = grouped[name][:].rearrange("p (t g i j) -> p g t i j", t=4, i=4, j=PACK)[:, :, t0:t1]
+            nc.gpsimd.tensor_scalar(dest, raw[name][:].rearrange("p j (g t i) -> p g t i j", t=4, i=4)[:, :, t0:t1], 1.0, 0.0, ALU.mult, ALU.add)
 
         def quantize_weights(name):
             nc.vector.quantize_mx(out=w_words[name][:].bitcast(FP8X4), scales=w_scales[name][:], in_=grouped[name][:])
@@ -95,7 +96,7 @@ def tile_picked_zlink_reluxsoft_p_kernel(tc, x_words, x_scales, w1, w2, offs, ds
 
         d_words = keep.tile([P, V], U32, name="d_words", align_bytes=64)
         d_scales = keep.tile([P, V], U8, name="d_scales", align_bytes=64)
-        d_hidden = [keep.tile([P, HALF * PACK], BF16, name=f"d_hidden{h}", align_bytes=64) for h in range(2)]
+        d_hidden = {0: keep.tile([P, HALF * PACK], BF16, name="d_hidden_early", align_bytes=64)}
         p_hidden = [keep.tile([P, CHUNK * PACK], BF16, name=f"p_hidden{c}", align_bytes=64) for c in range(CHUNKS)]
         p_words = [keep.tile([P, CHUNK], U32, name=f"p_words{c}", align_bytes=64) for c in range(CHUNKS)]
         p_scales = [keep.tile([P, CHUNK], U8, name=f"p_scales{c}", align_bytes=64) for c in range(CHUNKS)]
@@ -149,34 +150,34 @@ def tile_picked_zlink_reluxsoft_p_kernel(tc, x_words, x_scales, w1, w2, offs, ds
 
         nc.vector.memset(scale_table[:].bitcast(I32), 0)
         nc.sync.dma_start(dst_list[:], dst)
-        for q in range(4):
-            load_scales(q, nc.scalar)
         load_words(nc.sync)
-        load_weights("w2", 0, nc.sync)
+        for q in range(4):
+            load_scales(q, nc.sync)
+        load_weights("w2", nc.sync)
         nc.sync.dma_start(src_list[:], offs)
-        load_weights("w2", 1, nc.sync)
-        load_weights("w1", 0, nc.sync)
-        load_weights("w1", 1, nc.sync)
+        load_weights("w1", nc.sync)
 
-        xd_scales = gather_scales("xd_scales", dst_list)
-        xd_words = gather_words("xd_words", dst_list[:], "xd_words")
-        round_weights("w2", 0, nc.scalar.copy, 0, 3)
-        round_weights_gpsimd("w2", 0, 3, 4)
-        round_weights("w2", 1, nc.scalar.copy, 0, 3)
-        round_weights_gpsimd("w2", 1, 3, 4)
-        xs_scales = gather_scales("xs_scales", src_list)
-        round_weights("w1", 0, nc.scalar.copy, 0, 2)
-        round_weights_gpsimd("w1", 0, 2, 4)
+        xd_words = gather_words("xd_words", dst_list[:])
+        xd_scales = gather_scales("xd_scales", dst_list[:])
+        xs_words = [gather_words("xs_words0", src_list[:, 0:16])]
+        round_weights("w2", nc.vector.tensor_copy, 0, 1)
+        round_weights("w2", nc.scalar.copy, 1, 3)
+        round_weights_gpsimd("w2", 3, 4)
         quantize_weights("w2")
-        xs_words = [gather_words("xs_words0", src_list[:, 0:16], "raw_w2_1")]
         d_banks = [hidden_matmuls("w2", chunk(xd_words, c), chunk(xd_scales, c)) for c in range(CHUNKS)]
-        round_weights("w1", 1, nc.vector.tensor_copy)
+        xs_scales = gather_scales("xs_scales", src_list[:], 0)
+        round_weights("w1", nc.vector.tensor_copy, 0, 1)
+        round_weights("w1", nc.scalar.copy, 1, 3)
+        round_weights_gpsimd("w1", 3, 4)
         quantize_weights("w1")
-        xs_words.append(gather_words("xs_words1", src_list[:, 16:32], "grouped_w1"))
-        for c in range(CHUNKS):
-            relu(d_part(c), d_banks[c])
-            if c % 2 == 1:
-                quantize_d(c // 2)
+        xs_words.append(gather_words("xs_words1", src_list[:, 16:32], 4096))
+        d_hidden[1] = shared.tile([P, HALF * PACK], BF16, name="d_hidden_late", align_bytes=64, offset=4096 + 1024)
+        relu(d_part(0), d_banks[0])
+        relu(d_part(1), d_banks[1])
+        relu_vector(d_part(3), d_banks[3])
+        relu(d_part(2), d_banks[2])
+        quantize_d(0)
+        quantize_d(1)
         for c in range(CHUNKS):
             bank = hidden_matmuls("w1", chunk(xs_words[c // 2], c % 2), chunk(xs_scales, c))
             relu(p_hidden[c][:], bank)
@@ -186,7 +187,7 @@ def tile_picked_zlink_reluxsoft_p_kernel(tc, x_words, x_scales, w1, w2, offs, ds
             row_max(c, score)
             exponentials(c, score)
             invert(c)
-            if c < 2:
+            if c < 1:
                 normalise_gpsimd(c)
             else:
                 normalise_vector(c)

@@ -149,8 +149,8 @@ def tile_picked_zlink_reluxsoft_p_kernel(tc, x_words, x_scales, w1, w2, offs, ds
             nc.sync.dma_start(out[c * CHUNK : (c + 1) * CHUNK, :], result[c][:])
 
         nc.vector.memset(scale_table[:].bitcast(I32), 0)
-        nc.sync.dma_start(dst_list[:], dst)
         load_words(nc.sync)
+        nc.sync.dma_start(dst_list[:], dst)
         for q in range(4):
             load_scales(q, nc.sync)
         load_weights("w2", nc.sync)

@@ -111,8 +111,8 @@ def tile_picked_zlink_reluxsoft_p_kernel(tc, x_words, x_scales, w1, w2, offs, ds
         def quantize_p(c):
             nc.vector.quantize_mx(out=p_words[c][:].bitcast(FP8X4), scales=p_scales[c][:], in_=p_hidden[c][:])
 
-        neg_max = [keep.tile([P, 1], F32, name=f"neg_max{c}") for c in range(CHUNKS)]
-        total = [keep.tile([P, 1], F32, name=f"total{c}") for c in range(CHUNKS)]
+        neg_max = {c: keep.tile([P, 1], F32, name=f"neg_max{c}") for c in range(2)}
+        total = {c: keep.tile([P, 1], F32, name=f"total{c}") for c in range(1, CHUNKS)}
         inverse = [keep.tile([P, 1], F32, name=f"inverse{c}") for c in range(CHUNKS)]
         powers = [keep.tile([P, V], F32, name=f"powers{c}") for c in range(CHUNKS)]
         result = [keep.tile([P, V], F32, name=f"result{c}") for c in range(CHUNKS)]
@@ -182,13 +182,18 @@ def tile_picked_zlink_reluxsoft_p_kernel(tc, x_words, x_scales, w1, w2, offs, ds
             bank = hidden_matmuls("w1", chunk(xs_words[c // 2], c % 2), chunk(xs_scales, c))
             relu(p_hidden[c][:], bank)
             quantize_p(c)
+        first_total = shared.tile([P, 16], F32, name="first_total", offset=8192)
+        total[0] = first_total[:, 0:1]
         for c in range(CHUNKS):
+            if c >= 2:
+                neg_max[c] = shared.tile([P, 1], F32, name=f"late_max{c}", offset=8192 + 32 * (c - 2))
             score = score_matmul(c)
             row_max(c, score)
             exponentials(c, score)
             invert(c)
-            if c < 1:
+            if c == 0:
                 normalise_gpsimd(c)
-            else:
-                normalise_vector(c)
+                store(c)
+        for c in range(1, CHUNKS):
+            normalise_vector(c)
             store(c)

@@ -167,9 +167,12 @@ def tile_picked_zlink_reluxsoft_p_kernel(tc, x_words, x_scales, w1, w2, offs, ds
         d_banks = [hidden_matmuls("w2", chunk(xd_words, c), chunk(xd_scales, c)) for c in range(CHUNKS)]
         xs_scales = gather_scales("xs_scales", src_list[:], 0)
         round_weights("w1", nc.vector.tensor_copy, 0, 1)
-        round_weights("w1", nc.scalar.copy, 1, 3)
+        round_weights("w1", nc.scalar.copy, 1, 2)
+        round_weights("w1", nc.scalar.copy, 2, 3)
         round_weights_gpsimd("w1", 3, 4)
-        quantize_weights("w1")
+        for h in range(2):
+            cols = slice(h * HALF, (h + 1) * HALF)
+            nc.vector.quantize_mx(out=w_words["w1"][:, cols].bitcast(FP8X4), scales=w_scales["w1"][:, cols], in_=grouped["w1"][:, h * HALF * PACK : (h + 1) * HALF * PACK])
         xs_words.append(gather_words("xs_words1", src_list[:, 16:32], 4096))
         d_hidden[1] = shared.tile([P, HALF * PACK], BF16, name="d_hidden_late", align_bytes=64, offset=4096 + 1024)
         relu(d_part(0), d_banks[0])
@@ -194,6 +197,11 @@ def tile_picked_zlink_reluxsoft_p_kernel(tc, x_words, x_scales, w1, w2, offs, ds
             if c == 0:
                 normalise_gpsimd(c)
                 store(c)
-        for c in range(1, CHUNKS):
+        for c in range(1, CHUNKS - 1):
             normalise_vector(c)
             store(c)
+        c = CHUNKS - 1
+        for h in range(2):
+            cols = slice(h * HALF, (h + 1) * HALF)
+            nc.vector.tensor_scalar(result[c][:, cols], powers[c][:, cols], inverse[c][:], None, ALU.mult)
+            nc.sync.dma_start(out[c * CHUNK : (c + 1) * CHUNK, cols], result[c][:, cols])

@@ -149,40 +149,43 @@ def tile_picked_zlink_reluxsoft_p_kernel(tc, x_words, x_scales, w1, w2, offs, ds
             nc.sync.dma_start(out[c * CHUNK : (c + 1) * CHUNK, :], result[c][:])
 
         nc.vector.memset(scale_table[:].bitcast(I32), 0)
-        load_words(nc.sync)
+        w2_rows = w2.rearrange("(p j) c -> p j c", j=PACK)
+        nc.sync.dma_start(raw["w2"][:, 0:1], w2_rows[:, 0:1])
         nc.sync.dma_start(dst_list[:], dst)
-        for q in range(4):
-            load_scales(q, nc.sync)
-        load_weights("w2", nc.sync)
         nc.sync.dma_start(src_list[:], offs)
+        load_scales(0, nc.sync)
+        load_scales(1, nc.sync)
+        load_scales(2, nc.scalar)
+        load_scales(3, nc.scalar)
+        nc.sync.dma_start(raw["w2"][:, 1:PACK], w2_rows[:, 1:PACK])
+        load_words(nc.sync)
         load_weights("w1", nc.sync)
 
-        xd_words = gather_words("xd_words", dst_list[:])
+        warm = keep.tile([P, 2], F32, name="warm")
+        nc.gpsimd.memset(warm[:, 0:1], 0.0)
+        nc.scalar.activation(warm[:, 1:2], warm[:, 0:1], ACT.Exp)
         xd_scales = gather_scales("xd_scales", dst_list[:])
-        xs_words = [gather_words("xs_words0", src_list[:, 0:16])]
-        round_weights("w2", nc.vector.tensor_copy, 0, 1)
-        round_weights("w2", nc.scalar.copy, 1, 3)
-        round_weights_gpsimd("w2", 3, 4)
+        xs_scales = gather_scales("xs_scales", src_list[:])
+        xd_words = [gather_words("xd_words0", dst_list[:, 0:16])]
+        round_weights("w2", nc.scalar.copy, 0, 2)
+        round_weights_gpsimd("w2", 2, 4)
         quantize_weights("w2")
-        d_banks = [hidden_matmuls("w2", chunk(xd_words, c), chunk(xd_scales, c)) for c in range(CHUNKS)]
-        xs_scales = gather_scales("xs_scales", src_list[:], 0)
-        round_weights("w1", nc.vector.tensor_copy, 0, 1)
+        xd_words.append(gather_words("xd_words1", dst_list[:, 16:32], 0))
+        xs_words = gather_words("xs_words", src_list[:], 1024)
+        d_banks = [hidden_matmuls("w2", chunk(xd_words[c // 2], c % 2), chunk(xd_scales, c)) for c in range(CHUNKS)]
+        d_all = keep.tile([P, V * PACK], BF16, name="d_all", align_bytes=64)
+        relu(d_all[:, 0:512], d_banks[0])
+        round_weights_gpsimd("w1", 0, 1)
         round_weights("w1", nc.scalar.copy, 1, 2)
-        round_weights("w1", nc.scalar.copy, 2, 3)
-        round_weights_gpsimd("w1", 3, 4)
+        round_weights("w1", nc.vector.tensor_copy, 2, 4)
         for h in range(2):
             cols = slice(h * HALF, (h + 1) * HALF)
             nc.vector.quantize_mx(out=w_words["w1"][:, cols].bitcast(FP8X4), scales=w_scales["w1"][:, cols], in_=grouped["w1"][:, h * HALF * PACK : (h + 1) * HALF * PACK])
-        xs_words.append(gather_words("xs_words1", src_list[:, 16:32], 4096))
-        d_hidden[1] = shared.tile([P, HALF * PACK], BF16, name="d_hidden_late", align_bytes=64, offset=4096 + 1024)
-        relu(d_part(0), d_banks[0])
-        relu(d_part(1), d_banks[1])
-        relu_vector(d_part(3), d_banks[3])
-        relu(d_part(2), d_banks[2])
-        quantize_d(0)
-        quantize_d(1)
+        for c in range(1, CHUNKS):
+            relu(d_all[:, c * 512 : (c + 1) * 512], d_banks[c])
+        nc.vector.quantize_mx(out=d_words[:].bitcast(FP8X4), scales=d_scales[:], in_=d_all[:])
         for c in range(CHUNKS):
-            bank = hidden_matmuls("w1", chunk(xs_words[c // 2], c % 2), chunk(xs_scales, c))
+            bank = hidden_matmuls("w1", chunk(xs_words, c), chunk(xs_scales, c))
             relu(p_hidden[c][:], bank)
             quantize_p(c)
         first_total = shared.tile([P, 16], F32, name="first_total", offset=8192)

@@ -162,30 +162,33 @@ def tile_picked_zlink_reluxsoft_p_kernel(tc, x_words, x_scales, w1, w2, offs, ds
         load_weights("w1", nc.sync)
 
         warm = keep.tile([P, 2], F32, name="warm")
-        nc.gpsimd.memset(warm[:, 0:1], 0.0)
+        nc.vector.memset(warm[:, 0:1], 0.0)
         nc.scalar.activation(warm[:, 1:2], warm[:, 0:1], ACT.Exp)
         xd_scales = gather_scales("xd_scales", dst_list[:])
         xs_scales = gather_scales("xs_scales", src_list[:])
-        xd_words = [gather_words("xd_words0", dst_list[:, 0:16])]
         round_weights("w2", nc.scalar.copy, 0, 2)
         round_weights_gpsimd("w2", 2, 4)
+        xd_first = gather_words("xd_words_first", dst_list[:, 0:16])
         quantize_weights("w2")
-        xd_words.append(gather_words("xd_words1", dst_list[:, 16:32], 0))
-        xs_words = gather_words("xs_words", src_list[:], 1024)
-        d_banks = [hidden_matmuls("w2", chunk(xd_words[c // 2], c % 2), chunk(xd_scales, c)) for c in range(CHUNKS)]
-        d_all = keep.tile([P, V * PACK], BF16, name="d_all", align_bytes=64)
-        relu(d_all[:, 0:512], d_banks[0])
-        round_weights_gpsimd("w1", 0, 1)
-        round_weights("w1", nc.scalar.copy, 1, 2)
+        xd_rest = gather_words("xd_words_rest", dst_list[:, 16:32], 0)
+        xd_words = [chunk(xd_first, 0), chunk(xd_first, 1), chunk(xd_rest, 0), chunk(xd_rest, 1)]
+        xs_words = [gather_words("xs_words0", src_list[:, 0:16], 2048)]
+        d_banks = [hidden_matmuls("w2", xd_words[c], chunk(xd_scales, c)) for c in range(CHUNKS)]
+        relu(d_part(0), d_banks[0])
+        round_weights("w1", nc.vector.tensor_copy, 0, 2)
         round_weights("w1", nc.vector.tensor_copy, 2, 4)
         for h in range(2):
             cols = slice(h * HALF, (h + 1) * HALF)
             nc.vector.quantize_mx(out=w_words["w1"][:, cols].bitcast(FP8X4), scales=w_scales["w1"][:, cols], in_=grouped["w1"][:, h * HALF * PACK : (h + 1) * HALF * PACK])
-        for c in range(1, CHUNKS):
-            relu(d_all[:, c * 512 : (c + 1) * 512], d_banks[c])
-        nc.vector.quantize_mx(out=d_words[:].bitcast(FP8X4), scales=d_scales[:], in_=d_all[:])
+        xs_words.append(gather_words("xs_words1", src_list[:, 16:32], 4096))
+        d_hidden[1] = keep.tile([P, HALF * PACK], BF16, name="d_hidden_late", align_bytes=64)
+        relu(d_part(1), d_banks[1])
+        relu(d_part(2), d_banks[2])
+        relu(d_part(3), d_banks[3])
+        quantize_d(0)
+        quantize_d(1)
         for c in range(CHUNKS):
-            bank = hidden_matmuls("w1", chunk(xs_words, c), chunk(xs_scales, c))
+            bank = hidden_matmuls("w1", chunk(xs_words[c // 2], c % 2), chunk(xs_scales, c))
             relu(p_hidden[c][:], bank)
             quantize_p(c)
         first_total = shared.tile([P, 16], F32, name="first_total", offset=8192)
@@ -197,10 +200,10 @@ def tile_picked_zlink_reluxsoft_p_kernel(tc, x_words, x_scales, w1, w2, offs, ds
             row_max(c, score)
             exponentials(c, score)
             invert(c)
-            if c == 0:
+            if c <= 1:
                 normalise_gpsimd(c)
                 store(c)
-        for c in range(1, CHUNKS - 1):
+        for c in range(2, CHUNKS - 1):
             normalise_vector(c)
             store(c)
         c = CHUNKS - 1

@@ -20,6 +20,7 @@ PACK = 4
 CHUNK = 128
 CHUNKS = 4
 HALF = 256
+GROUPS = {"w2": [(0, 32)], "w1": [(0, 20), (20, 32)]}
 
 
 def tile_picked_zlink_reluxsoft_p_kernel(tc, x_words, x_scales, w1, w2, offs, dst, out):
@@ -33,20 +34,16 @@ def tile_picked_zlink_reluxsoft_p_kernel(tc, x_words, x_scales, w1, w2, offs, ds
         src_list = keep.tile([P, S // 16], U16, name="src_list")
         scale_table = keep.tile([P, T], U8, name="scale_table", align_bytes=64)
         word_table = keep.tile([P, T], I32, name="word_table", align_bytes=64)
-        raw = {n: keep.tile([P, PACK, H], F32, name=f"raw_{n}", align_bytes=64) for n in ("w1", "w2")}
-        weights = {"w1": w1, "w2": w2}
+        raw = {
+            "w2": [shared.tile([P, PACK, H], F32, name="raw_w2", align_bytes=64, offset=16384)],
+            "w1": [shared.tile([P, PACK, 16 * (g1 - g0)], F32, name=f"raw_w1_{g0}", align_bytes=64, offset=24576 + 256 * g0) for g0, g1 in GROUPS["w1"]],
+        }
 
         def load_scales(q, queue):
             queue.dma_start(scale_table[32 * q : 32 * q + 4, :].bitcast(I32), x_scales[0, 4 * q : 4 * q + 4, :].bitcast(I32))
 
-        def load_words(queue):
-            queue.dma_start(word_table[:], x_words[0].rearrange("p c r -> p (c r)").bitcast(I32))
-
-        def load_weights(name, queue):
-            queue.dma_start(raw[name][:], weights[name].rearrange("(p j) c -> p j c", j=PACK))
-
-        def gather_scales(name, offsets, at=None):
-            scales = (keep if at is None else shared).tile([P, 16 * offsets.shape[1]], U8, name=name, align_bytes=64, offset=at)
+        def gather_scales(name, offsets):
+            scales = keep.tile([P, 16 * offsets.shape[1]], U8, name=name, align_bytes=64)
             nc.vector.tensor_copy(scales[:], scale_table[:].indirect(offsets))
             return scales
 
@@ -55,24 +52,29 @@ def tile_picked_zlink_reluxsoft_p_kernel(tc, x_words, x_scales, w1, w2, offs, ds
             nc.vector.tensor_copy(words[:], word_table[:].bitcast(U32).indirect(offsets))
             return words
 
-        grouped = {n: shared.tile([P, H * PACK], BF16, name=f"grouped_{n}", align_bytes=64, offset=at) for n, at in (("w2", 0), ("w1", 4096))}
+        rounded = {
+            n: [shared.tile([P, HALF * PACK], BF16, name=f"rounded_{n}_{u}", align_bytes=64, offset=at + 2048 * u) for u in range(2)]
+            for n, at in (("w2", 0), ("w1", 4096))
+        }
         w_words = {n: keep.tile([P, H], U32, name=f"words_{n}", align_bytes=64) for n in ("w1", "w2")}
         w_scales = {n: keep.tile([P, H], U8, name=f"scales_{n}", align_bytes=64) for n in ("w1", "w2")}
 
-        def round_weights(name, copy, t0, t1):
-            dest = grouped[name][:].rearrange("p (t g i j) -> p t g j i", t=4, i=4, j=PACK)[:, t0:t1]
-            copy(dest, raw[name][:].rearrange("p j (g t i) -> p t g j i", t=4, i=4)[:, t0:t1])
+        def round_tiles(name, piece, copy, t0, t1):
+            g0, g1 = GROUPS[name][piece]
+            dest = rounded[name][t0 // 2][:].rearrange("p (t g i j) -> p t g j i", t=2, i=4, j=PACK)[:, t0 % 2 : t0 % 2 + t1 - t0, g0:g1]
+            copy(dest, raw[name][piece][:].rearrange("p j (g t i) -> p t g j i", t=4, i=4)[:, t0:t1])
 
-        def round_weights_gpsimd(name, t0, t1):
-            dest = grouped[name][:].rearrange("p (t g i j) -> p g t i j", t=4, i=4, j=PACK)[:, :, t0:t1]
-            nc.gpsimd.tensor_scalar(dest, raw[name][:].rearrange("p j (g t i) -> p g t i j", t=4, i=4)[:, :, t0:t1], 1.0, 0.0, ALU.mult, ALU.add)
+        def round_tiles_gpsimd(name, piece, t0, t1):
+            g0, g1 = GROUPS[name][piece]
+            dest = rounded[name][t0 // 2][:].rearrange("p (t g i j) -> p g t i j", t=2, i=4, j=PACK)[:, g0:g1, t0 % 2 : t0 % 2 + t1 - t0]
+            nc.gpsimd.tensor_scalar(dest, raw[name][piece][:].rearrange("p j (g t i) -> p g t i j", t=4, i=4)[:, :, t0:t1], 1.0, 0.0, ALU.mult, ALU.add)
 
-        def quantize_weights(name):
-            nc.vector.quantize_mx(out=w_words[name][:].bitcast(FP8X4), scales=w_scales[name][:], in_=grouped[name][:])
+        def quantize_weights(name, u):
+            cols = slice(u * HALF, (u + 1) * HALF)
+            nc.vector.quantize_mx(out=w_words[name][:, cols].bitcast(FP8X4), scales=w_scales[name][:, cols], in_=rounded[name][u][:])
 
-        def hidden_matmuls(name, words, scales):
-            bank = psum.tile([P, PACK, CHUNK], F32, name="hid_bank", tag="bank")
-            for t in range(PACK):
+        def hidden_matmuls(bank, name, words, scales, t0, t1):
+            for t in range(t0, t1):
                 cols = slice(t * P, (t + 1) * P)
                 nc.tensor.matmul_mx(
                     out=bank[:, t, :],
@@ -83,7 +85,6 @@ def tile_picked_zlink_reluxsoft_p_kernel(tc, x_words, x_scales, w1, w2, offs, ds
                     start=True,
                     stop=True,
                 )
-            return bank
 
         def relu(hidden, bank):
             nc.scalar.activation(hidden.rearrange("p (n t) -> p n t", t=PACK), bank[:].rearrange("p t n -> p n t"), ACT.Relu)
@@ -96,7 +97,7 @@ def tile_picked_zlink_reluxsoft_p_kernel(tc, x_words, x_scales, w1, w2, offs, ds
 
         d_words = keep.tile([P, V], U32, name="d_words", align_bytes=64)
         d_scales = keep.tile([P, V], U8, name="d_scales", align_bytes=64)
-        d_hidden = {0: keep.tile([P, HALF * PACK], BF16, name="d_hidden_early", align_bytes=64)}
+        d_hidden = [keep.tile([P, HALF * PACK], BF16, name=f"d_hidden{h}", align_bytes=64) for h in range(2)]
         p_hidden = [keep.tile([P, CHUNK * PACK], BF16, name=f"p_hidden{c}", align_bytes=64) for c in range(CHUNKS)]
         p_words = [keep.tile([P, CHUNK], U32, name=f"p_words{c}", align_bytes=64) for c in range(CHUNKS)]
         p_scales = [keep.tile([P, CHUNK], U8, name=f"p_scales{c}", align_bytes=64) for c in range(CHUNKS)]
@@ -150,45 +151,55 @@ def tile_picked_zlink_reluxsoft_p_kernel(tc, x_words, x_scales, w1, w2, offs, ds
 
         nc.vector.memset(scale_table[:].bitcast(I32), 0)
         w2_rows = w2.rearrange("(p j) c -> p j c", j=PACK)
-        nc.sync.dma_start(raw["w2"][:, 0:1], w2_rows[:, 0:1])
+        w1_rows = w1.rearrange("(p j) c -> p j c", j=PACK)
+        nc.sync.dma_start(raw["w2"][0][:, 0:1], w2_rows[:, 0:1])
         nc.sync.dma_start(dst_list[:], dst)
         nc.sync.dma_start(src_list[:], offs)
         load_scales(0, nc.sync)
         load_scales(1, nc.sync)
         load_scales(2, nc.scalar)
         load_scales(3, nc.scalar)
-        nc.sync.dma_start(raw["w2"][:, 1:PACK], w2_rows[:, 1:PACK])
-        load_words(nc.sync)
-        load_weights("w1", nc.sync)
+        nc.sync.dma_start(raw["w2"][0][:, 1:PACK], w2_rows[:, 1:PACK])
+        nc.sync.dma_start(word_table[:], x_words[0].rearrange("p c r -> p (c r)").bitcast(I32))
+        for h, (g0, g1) in enumerate(GROUPS["w1"]):
+            nc.sync.dma_start(raw["w1"][h][:], w1_rows[:, :, 16 * g0 : 16 * g1])
 
         warm = keep.tile([P, 2], F32, name="warm")
         nc.vector.memset(warm[:, 0:1], 0.0)
         nc.scalar.activation(warm[:, 1:2], warm[:, 0:1], ACT.Exp)
+
         xd_scales = gather_scales("xd_scales", dst_list[:])
         xs_scales = gather_scales("xs_scales", src_list[:])
-        round_weights("w2", nc.scalar.copy, 0, 2)
-        round_weights_gpsimd("w2", 2, 4)
-        xd_first = gather_words("xd_words_first", dst_list[:, 0:16])
-        quantize_weights("w2")
-        xd_rest = gather_words("xd_words_rest", dst_list[:, 16:32], 0)
-        xd_words = [chunk(xd_first, 0), chunk(xd_first, 1), chunk(xd_rest, 0), chunk(xd_rest, 1)]
-        xs_words = [gather_words("xs_words0", src_list[:, 0:16], 2048)]
-        d_banks = [hidden_matmuls("w2", xd_words[c], chunk(xd_scales, c)) for c in range(CHUNKS)]
+        round_tiles("w2", 0, nc.scalar.copy, 0, 2)
+        round_tiles_gpsimd("w2", 0, 2, 4)
+        xd_first = gather_words("xd_first", dst_list[:, 0:8])
+        warm_bank = psum.tile([P, PACK, CHUNK], F32, name="warm_bank", tag="bank")
+        for n in range(2):
+            nc.tensor.matmul_mx(out=warm_bank[:, n, :], lhsT=chunk(xd_first, 0).bitcast(FP8X4), lhsT_scale=chunk(xd_scales, 0), rhs=chunk(xd_first, 0).bitcast(FP8X4), rhs_scale=chunk(xd_scales, 0), start=True, stop=True)
+        quantize_weights("w2", 0)
+        quantize_weights("w2", 1)
+        xd_second = gather_words("xd_second", dst_list[:, 8:16], 16384 + 2048)
+        xd_rest = gather_words("xd_rest", dst_list[:, 16:32], 16384)
+        xd_words = [xd_first[:], xd_second[:], chunk(xd_rest, 0), chunk(xd_rest, 1)]
+        xs_words = [gather_words("xs_first", src_list[:, 0:16], 16384 + 1024)]
+        d_banks = [psum.tile([P, PACK, CHUNK], F32, name=f"d_bank{c}", tag="bank") for c in range(CHUNKS)]
+        for c in range(CHUNKS):
+            hidden_matmuls(d_banks[c], "w2", xd_words[c], chunk(xd_scales, c), 0, PACK)
+        round_tiles("w1", 0, nc.scalar.copy, 0, 2)
+        round_tiles_gpsimd("w1", 0, 2, 4)
         relu(d_part(0), d_banks[0])
-        round_weights("w1", nc.vector.tensor_copy, 0, 2)
-        round_weights("w1", nc.vector.tensor_copy, 2, 4)
-        for h in range(2):
-            cols = slice(h * HALF, (h + 1) * HALF)
-            nc.vector.quantize_mx(out=w_words["w1"][:, cols].bitcast(FP8X4), scales=w_scales["w1"][:, cols], in_=grouped["w1"][:, h * HALF * PACK : (h + 1) * HALF * PACK])
-        xs_words.append(gather_words("xs_words1", src_list[:, 16:32], 4096))
-        d_hidden[1] = keep.tile([P, HALF * PACK], BF16, name="d_hidden_late", align_bytes=64)
-        relu(d_part(1), d_banks[1])
-        relu(d_part(2), d_banks[2])
-        relu(d_part(3), d_banks[3])
+        round_tiles("w1", 1, nc.vector.tensor_copy, 0, 2)
+        round_tiles("w1", 1, nc.vector.tensor_copy, 2, 4)
+        quantize_weights("w1", 0)
+        quantize_weights("w1", 1)
+        xs_words.append(gather_words("xs_rest", src_list[:, 16:32], 24576 + 256 * 20))
+        for c in range(1, CHUNKS):
+            relu(d_part(c), d_banks[c])
         quantize_d(0)
         quantize_d(1)
         for c in range(CHUNKS):
-            bank = hidden_matmuls("w1", chunk(xs_words[c // 2], c % 2), chunk(xs_scales, c))
+            bank = psum.tile([P, PACK, CHUNK], F32, name="p_bank", tag="bank")
+            hidden_matmuls(bank, "w1", chunk(xs_words[c // 2], c % 2), chunk(xs_scales, c), 0, PACK)
             relu(p_hidden[c][:], bank)
             quantize_p(c)
         first_total = shared.tile([P, 16], F32, name="first_total", offset=8192)
@@ -200,7 +211,7 @@ def tile_picked_zlink_reluxsoft_p_kernel(tc, x_words, x_scales, w1, w2, offs, ds
             row_max(c, score)
             exponentials(c, score)
             invert(c)
-            if c <= 1:
+            if c < 2:
                 normalise_gpsimd(c)
                 store(c)
         for c in range(2, CHUNKS - 1):

@@ -97,17 +97,13 @@ def tile_picked_zlink_reluxsoft_p_kernel(tc, x_words, x_scales, w1, w2, offs, ds
 
         d_words = keep.tile([P, V], U32, name="d_words", align_bytes=64)
         d_scales = keep.tile([P, V], U8, name="d_scales", align_bytes=64)
-        d_hidden = [keep.tile([P, HALF * PACK], BF16, name=f"d_hidden{h}", align_bytes=64) for h in range(2)]
+        d_hidden = keep.tile([P, V * PACK], BF16, name="d_hidden", align_bytes=64)
         p_hidden = [keep.tile([P, CHUNK * PACK], BF16, name=f"p_hidden{c}", align_bytes=64) for c in range(CHUNKS)]
         p_words = [keep.tile([P, CHUNK], U32, name=f"p_words{c}", align_bytes=64) for c in range(CHUNKS)]
         p_scales = [keep.tile([P, CHUNK], U8, name=f"p_scales{c}", align_bytes=64) for c in range(CHUNKS)]
 
         def d_part(c):
-            return d_hidden[c // 2][:, (c % 2) * CHUNK * PACK : (c % 2 + 1) * CHUNK * PACK]
-
-        def quantize_d(h):
-            cols = slice(h * HALF, (h + 1) * HALF)
-            nc.vector.quantize_mx(out=d_words[:, cols].bitcast(FP8X4), scales=d_scales[:, cols], in_=d_hidden[h][:])
+            return d_hidden[:, c * CHUNK * PACK : (c + 1) * CHUNK * PACK]
 
         def quantize_p(c):
             nc.vector.quantize_mx(out=p_words[c][:].bitcast(FP8X4), scales=p_scales[c][:], in_=p_hidden[c][:])
@@ -150,31 +146,33 @@ def tile_picked_zlink_reluxsoft_p_kernel(tc, x_words, x_scales, w1, w2, offs, ds
             nc.sync.dma_start(out[c * CHUNK : (c + 1) * CHUNK, :], result[c][:])
 
         nc.vector.memset(scale_table[:].bitcast(I32), 0)
-        w2_rows = w2.rearrange("(p j) c -> p j c", j=PACK)
         w1_rows = w1.rearrange("(p j) c -> p j c", j=PACK)
-        nc.sync.dma_start(raw["w2"][0][:, 0:1], w2_rows[:, 0:1])
+        w2_flat = raw["w2"][0][:].rearrange("p j c -> p (j c)")
+        w2_runs = w2.rearrange("(p j) c -> p (j c)", j=PACK)
+        nc.sync.dma_start(w2_flat[:, 0:640], w2_runs[:, 0:640])
         nc.sync.dma_start(dst_list[:], dst)
         nc.sync.dma_start(src_list[:], offs)
         load_scales(0, nc.sync)
         load_scales(1, nc.sync)
         load_scales(2, nc.scalar)
         load_scales(3, nc.scalar)
-        nc.sync.dma_start(raw["w2"][0][:, 1:PACK], w2_rows[:, 1:PACK])
+        nc.sync.dma_start(w2_flat[:, 640:], w2_runs[:, 640:])
         nc.sync.dma_start(word_table[:], x_words[0].rearrange("p c r -> p (c r)").bitcast(I32))
         for h, (g0, g1) in enumerate(GROUPS["w1"]):
             nc.sync.dma_start(raw["w1"][h][:], w1_rows[:, :, 16 * g0 : 16 * g1])
 
-        warm = keep.tile([P, 2], F32, name="warm")
-        nc.vector.memset(warm[:, 0:1], 0.0)
-        nc.scalar.activation(warm[:, 1:2], warm[:, 0:1], ACT.Exp)
-
         xd_scales = gather_scales("xd_scales", dst_list[:])
         xs_scales = gather_scales("xs_scales", src_list[:])
-        round_tiles("w2", 0, nc.scalar.copy, 0, 2)
+        first_dest = rounded["w2"][0][:].rearrange("p (t g i j) -> p t g j i", t=2, i=4, j=PACK)
+        first_rows = raw["w2"][0][:].rearrange("p j (g t i) -> p t g j i", t=4, i=4)
+        nc.scalar.copy(first_dest[:, 0, 0, 0:1], first_rows[:, 0, 0, 0:1])
+        nc.scalar.copy(first_dest[:, 0, 0, 1:PACK], first_rows[:, 0, 0, 1:PACK])
+        nc.scalar.copy(first_dest[:, 0, 1:], first_rows[:, 0, 1:])
+        nc.scalar.copy(first_dest[:, 1], first_rows[:, 1])
         round_tiles_gpsimd("w2", 0, 2, 4)
         xd_first = gather_words("xd_first", dst_list[:, 0:8])
         warm_bank = psum.tile([P, PACK, CHUNK], F32, name="warm_bank", tag="bank")
-        for n in range(2):
+        for n in range(3):
             nc.tensor.matmul_mx(out=warm_bank[:, n, :], lhsT=chunk(xd_first, 0).bitcast(FP8X4), lhsT_scale=chunk(xd_scales, 0), rhs=chunk(xd_first, 0).bitcast(FP8X4), rhs_scale=chunk(xd_scales, 0), start=True, stop=True)
         quantize_weights("w2", 0)
         quantize_weights("w2", 1)
@@ -195,8 +193,7 @@ def tile_picked_zlink_reluxsoft_p_kernel(tc, x_words, x_scales, w1, w2, offs, ds
         xs_words.append(gather_words("xs_rest", src_list[:, 16:32], 24576 + 256 * 20))
         for c in range(1, CHUNKS):
             relu(d_part(c), d_banks[c])
-        quantize_d(0)
-        quantize_d(1)
+        nc.vector.quantize_mx(out=d_words[:].bitcast(FP8X4), scales=d_scales[:], in_=d_hidden[:])
         for c in range(CHUNKS):
             bank = psum.tile([P, PACK, CHUNK], F32, name="p_bank", tag="bank")
             hidden_matmuls(bank, "w1", chunk(xs_words[c // 2], c % 2), chunk(xs_scales, c), 0, PACK)

@@ -171,9 +171,6 @@ def tile_picked_zlink_reluxsoft_p_kernel(tc, x_words, x_scales, w1, w2, offs, ds
         nc.scalar.copy(first_dest[:, 1], first_rows[:, 1])
         round_tiles_gpsimd("w2", 0, 2, 4)
         xd_first = gather_words("xd_first", dst_list[:, 0:8])
-        warm_bank = psum.tile([P, PACK, CHUNK], F32, name="warm_bank", tag="bank")
-        for n in range(3):
-            nc.tensor.matmul_mx(out=warm_bank[:, n, :], lhsT=chunk(xd_first, 0).bitcast(FP8X4), lhsT_scale=chunk(xd_scales, 0), rhs=chunk(xd_first, 0).bitcast(FP8X4), rhs_scale=chunk(xd_scales, 0), start=True, stop=True)
         quantize_weights("w2", 0)
         quantize_weights("w2", 1)
         xd_second = gather_words("xd_second", dst_list[:, 8:16], 16384 + 2048)

@@ -20,7 +20,7 @@ PACK = 4
 CHUNK = 128
 CHUNKS = 4
 HALF = 256
-GROUPS = {"w2": [(0, 32)], "w1": [(0, 20), (20, 32)]}
+GROUPS = {"w2": [(0, 32)], "w1": [(0, 16), (16, 32)]}
 
 
 def tile_picked_zlink_reluxsoft_p_kernel(tc, x_words, x_scales, w1, w2, offs, dst, out):
@@ -149,8 +149,8 @@ def tile_picked_zlink_reluxsoft_p_kernel(tc, x_words, x_scales, w1, w2, offs, ds
         w1_rows = w1.rearrange("(p j) c -> p j c", j=PACK)
         w2_flat = raw["w2"][0][:].rearrange("p j c -> p (j c)")
         w2_runs = w2.rearrange("(p j) c -> p (j c)", j=PACK)
-        nc.sync.dma_start(w2_flat[:, 0:640], w2_runs[:, 0:640])
         nc.sync.dma_start(dst_list[:], dst)
+        nc.sync.dma_start(w2_flat[:, 0:640], w2_runs[:, 0:640])
         nc.sync.dma_start(src_list[:], offs)
         load_scales(0, nc.sync)
         load_scales(1, nc.sync)
@@ -176,7 +176,7 @@ def tile_picked_zlink_reluxsoft_p_kernel(tc, x_words, x_scales, w1, w2, offs, ds
         xd_second = gather_words("xd_second", dst_list[:, 8:16], 16384 + 2048)
         xd_rest = gather_words("xd_rest", dst_list[:, 16:32], 16384)
         xd_words = [xd_first[:], xd_second[:], chunk(xd_rest, 0), chunk(xd_rest, 1)]
-        xs_words = [gather_words("xs_first", src_list[:, 0:16], 16384 + 1024)]
+        xs_first = gather_words("xs_first", src_list[:, 0:8], 16384 + 1024)
         d_banks = [psum.tile([P, PACK, CHUNK], F32, name=f"d_bank{c}", tag="bank") for c in range(CHUNKS)]
         for c in range(CHUNKS):
             hidden_matmuls(d_banks[c], "w2", xd_words[c], chunk(xd_scales, c), 0, PACK)
@@ -187,13 +187,15 @@ def tile_picked_zlink_reluxsoft_p_kernel(tc, x_words, x_scales, w1, w2, offs, ds
         round_tiles("w1", 1, nc.vector.tensor_copy, 2, 4)
         quantize_weights("w1", 0)
         quantize_weights("w1", 1)
-        xs_words.append(gather_words("xs_rest", src_list[:, 16:32], 24576 + 256 * 20))
+        xs_second = gather_words("xs_second", src_list[:, 8:16], 24576 + 256 * 16)
+        xs_rest = gather_words("xs_rest", src_list[:, 16:32], 24576 + 256 * 16 + 512)
+        xs_words = [xs_first[:], xs_second[:], chunk(xs_rest, 0), chunk(xs_rest, 1)]
         for c in range(1, CHUNKS):
             relu(d_part(c), d_banks[c])
         nc.vector.quantize_mx(out=d_words[:].bitcast(FP8X4), scales=d_scales[:], in_=d_hidden[:])
         for c in range(CHUNKS):
             bank = psum.tile([P, PACK, CHUNK], F32, name="p_bank", tag="bank")
-            hidden_matmuls(bank, "w1", chunk(xs_words[c // 2], c % 2), chunk(xs_scales, c), 0, PACK)
+            hidden_matmuls(bank, "w1", xs_words[c], chunk(xs_scales, c), 0, PACK)
             relu(p_hidden[c][:], bank)
             quantize_p(c)
         first_total = shared.tile([P, 16], F32, name="first_total", offset=8192)

@@ -169,7 +169,9 @@ def tile_picked_zlink_reluxsoft_p_kernel(tc, x_words, x_scales, w1, w2, offs, ds
         nc.scalar.copy(first_dest[:, 0, 0, 1:PACK], first_rows[:, 0, 0, 1:PACK])
         nc.scalar.copy(first_dest[:, 0, 1:], first_rows[:, 0, 1:])
         nc.scalar.copy(first_dest[:, 1], first_rows[:, 1])
-        round_tiles_gpsimd("w2", 0, 2, 4)
+        second_rows = raw["w2"][0][:].rearrange("p j (g t i) -> p g t i j", t=4, i=4)[:, 0:24, 2:4]
+        nc.gpsimd.tensor_scalar(rounded["w2"][1][:].rearrange("p (t g i j) -> p g t i j", t=2, i=4, j=PACK)[:, 0:24], second_rows, 1.0, 0.0, ALU.mult, ALU.add)
+        nc.scalar.copy(rounded["w2"][1][:].rearrange("p (t g i j) -> p t g j i", t=2, i=4, j=PACK)[:, :, 24:32], first_rows[:, 2:4, 24:32])
         xd_first = gather_words("xd_first", dst_list[:, 0:8])
         quantize_weights("w2", 0)
         quantize_weights("w2", 1)

@@ -89,9 +89,6 @@ def tile_picked_zlink_reluxsoft_p_kernel(tc, x_words, x_scales, w1, w2, offs, ds
         def relu(hidden, bank):
             nc.scalar.activation(hidden.rearrange("p (n t) -> p n t", t=PACK), bank[:].rearrange("p t n -> p n t"), ACT.Relu)
 
-        def relu_vector(hidden, bank):
-            nc.vector.tensor_scalar(hidden.rearrange("p (n t) -> p n t", t=PACK), bank[:].rearrange("p t n -> p n t"), 0.0, None, ALU.max)
-
         def chunk(tile, c):
             return tile[:, c * CHUNK : (c + 1) * CHUNK]
 
@@ -108,8 +105,8 @@ def tile_picked_zlink_reluxsoft_p_kernel(tc, x_words, x_scales, w1, w2, offs, ds
         def quantize_p(c):
             nc.vector.quantize_mx(out=p_words[c][:].bitcast(FP8X4), scales=p_scales[c][:], in_=p_hidden[c][:])
 
-        neg_max = {c: keep.tile([P, 1], F32, name=f"neg_max{c}") for c in range(2)}
-        total = {c: keep.tile([P, 1], F32, name=f"total{c}") for c in range(1, CHUNKS)}
+        neg_max = {}
+        total = {c: keep.tile([P, 1], F32, name=f"total{c}") for c in range(CHUNKS)}
         inverse = [keep.tile([P, 1], F32, name=f"inverse{c}") for c in range(CHUNKS)]
         powers = [keep.tile([P, V], F32, name=f"powers{c}") for c in range(CHUNKS)]
         result = [keep.tile([P, V], F32, name=f"result{c}") for c in range(CHUNKS)]
@@ -200,19 +197,16 @@ def tile_picked_zlink_reluxsoft_p_kernel(tc, x_words, x_scales, w1, w2, offs, ds
             hidden_matmuls(bank, "w1", xs_words[c], chunk(xs_scales, c), 0, PACK)
             relu(p_hidden[c][:], bank)
             quantize_p(c)
-        first_total = shared.tile([P, 16], F32, name="first_total", offset=8192)
-        total[0] = first_total[:, 0:1]
         for c in range(CHUNKS):
-            if c >= 2:
-                neg_max[c] = shared.tile([P, 1], F32, name=f"late_max{c}", offset=8192 + 32 * (c - 2))
+            neg_max[c] = shared.tile([P, 1], F32, name=f"neg_max{c}", offset=8192 + 32 * (c % 2))
             score = score_matmul(c)
             row_max(c, score)
             exponentials(c, score)
             invert(c)
-            if c < 2:
+            if c < 1:
                 normalise_gpsimd(c)
                 store(c)
-        for c in range(2, CHUNKS - 1):
+        for c in range(1, CHUNKS - 1):
             normalise_vector(c)
             store(c)
         c = CHUNKS - 1

@@ -32,32 +32,32 @@ def tile_picked_zlink_reluxsoft_p_kernel(tc, x_words, x_scales, w1, w2, offs, ds
 
         dst_list = keep.tile([P, V // 16], U16, name="dst_list")
         src_list = keep.tile([P, S // 16], U16, name="src_list")
-        scale_table = keep.tile([P, T], U8, name="scale_table", align_bytes=64)
-        word_table = keep.tile([P, T], I32, name="word_table", align_bytes=64)
+        scale_table = keep.tile([P, T], U8, name="scale_table", align_bytes=256)
+        word_table = keep.tile([P, T], I32, name="word_table", align_bytes=256)
         raw = {
-            "w2": [shared.tile([P, PACK, H], F32, name="raw_w2", align_bytes=64, offset=16384)],
-            "w1": [shared.tile([P, PACK, 16 * (g1 - g0)], F32, name=f"raw_w1_{g0}", align_bytes=64, offset=24576 + 256 * g0) for g0, g1 in GROUPS["w1"]],
+            "w2": [shared.tile([P, PACK, H], F32, name="raw_w2", align_bytes=256, offset=16384)],
+            "w1": [shared.tile([P, PACK, 16 * (g1 - g0)], F32, name=f"raw_w1_{g0}", align_bytes=256, offset=24576 + 256 * g0) for g0, g1 in GROUPS["w1"]],
         }
 
         def load_scales(q, queue):
             queue.dma_start(scale_table[32 * q : 32 * q + 4, :].bitcast(I32), x_scales[0, 4 * q : 4 * q + 4, :].bitcast(I32))
 
         def gather_scales(name, offsets):
-            scales = keep.tile([P, 16 * offsets.shape[1]], U8, name=name, align_bytes=64)
+            scales = keep.tile([P, 16 * offsets.shape[1]], U8, name=name, align_bytes=256)
             nc.vector.tensor_copy(scales[:], scale_table[:].indirect(offsets))
             return scales
 
         def gather_words(name, offsets, at=None):
-            words = (keep if at is None else shared).tile([P, 16 * offsets.shape[1]], U32, name=name, align_bytes=64, offset=at)
+            words = (keep if at is None else shared).tile([P, 16 * offsets.shape[1]], U32, name=name, align_bytes=256, offset=at)
             nc.vector.tensor_copy(words[:], word_table[:].bitcast(U32).indirect(offsets))
             return words
 
         rounded = {
-            n: [shared.tile([P, HALF * PACK], BF16, name=f"rounded_{n}_{u}", align_bytes=64, offset=at + 2048 * u) for u in range(2)]
+            n: [shared.tile([P, HALF * PACK], BF16, name=f"rounded_{n}_{u}", align_bytes=256, offset=at + 2048 * u) for u in range(2)]
             for n, at in (("w2", 0), ("w1", 4096))
         }
-        w_words = {n: keep.tile([P, H], U32, name=f"words_{n}", align_bytes=64) for n in ("w1", "w2")}
-        w_scales = {n: keep.tile([P, H], U8, name=f"scales_{n}", align_bytes=64) for n in ("w1", "w2")}
+        w_words = {n: keep.tile([P, H], U32, name=f"words_{n}", align_bytes=256) for n in ("w1", "w2")}
+        w_scales = {n: keep.tile([P, H], U8, name=f"scales_{n}", align_bytes=256) for n in ("w1", "w2")}
 
         def round_tiles(name, piece, copy, t0, t1):
             g0, g1 = GROUPS[name][piece]
@@ -92,12 +92,12 @@ def tile_picked_zlink_reluxsoft_p_kernel(tc, x_words, x_scales, w1, w2, offs, ds
         def chunk(tile, c):
             return tile[:, c * CHUNK : (c + 1) * CHUNK]
 
-        d_words = keep.tile([P, V], U32, name="d_words", align_bytes=64)
-        d_scales = keep.tile([P, V], U8, name="d_scales", align_bytes=64)
-        d_hidden = keep.tile([P, V * PACK], BF16, name="d_hidden", align_bytes=64)
-        p_hidden = [keep.tile([P, CHUNK * PACK], BF16, name=f"p_hidden{c}", align_bytes=64) for c in range(CHUNKS)]
-        p_words = [keep.tile([P, CHUNK], U32, name=f"p_words{c}", align_bytes=64) for c in range(CHUNKS)]
-        p_scales = [keep.tile([P, CHUNK], U8, name=f"p_scales{c}", align_bytes=64) for c in range(CHUNKS)]
+        d_words = keep.tile([P, V], U32, name="d_words", align_bytes=256)
+        d_scales = keep.tile([P, V], U8, name="d_scales", align_bytes=256)
+        d_hidden = keep.tile([P, V * PACK], BF16, name="d_hidden", align_bytes=256)
+        p_hidden = [keep.tile([P, CHUNK * PACK], BF16, name=f"p_hidden{c}", align_bytes=256) for c in range(CHUNKS)]
+        p_words = [keep.tile([P, CHUNK], U32, name=f"p_words{c}", align_bytes=256) for c in range(CHUNKS)]
+        p_scales = [keep.tile([P, CHUNK], U8, name=f"p_scales{c}", align_bytes=256) for c in range(CHUNKS)]
 
         def d_part(c):
             return d_hidden[:, c * CHUNK * PACK : (c + 1) * CHUNK * PACK]
@@ -108,8 +108,8 @@ def tile_picked_zlink_reluxsoft_p_kernel(tc, x_words, x_scales, w1, w2, offs, ds
         neg_max = {}
         total = {c: keep.tile([P, 1], F32, name=f"total{c}") for c in range(CHUNKS)}
         inverse = [keep.tile([P, 1], F32, name=f"inverse{c}") for c in range(CHUNKS)]
-        powers = [keep.tile([P, V], F32, name=f"powers{c}") for c in range(CHUNKS)]
-        result = [keep.tile([P, V], F32, name=f"result{c}") for c in range(CHUNKS)]
+        powers = [keep.tile([P, V], F32, name=f"powers{c}", align_bytes=256) for c in range(CHUNKS)]
+        result = [keep.tile([P, V], F32, name=f"result{c}", align_bytes=256) for c in range(CHUNKS)]
 
         def score_matmul(c):
             score = psum.tile([P, V], F32, name="score", tag="bank")

@@ -59,15 +59,17 @@ def tile_picked_zlink_reluxsoft_p_kernel(tc, x_words, x_scales, w1, w2, offs, ds
         w_words = {n: keep.tile([P, H], U32, name=f"words_{n}", align_bytes=256) for n in ("w1", "w2")}
         w_scales = {n: keep.tile([P, H], U8, name=f"scales_{n}", align_bytes=256) for n in ("w1", "w2")}
 
-        def round_tiles(name, piece, copy, t0, t1):
+        def round_views(name, piece, u, order):
             g0, g1 = GROUPS[name][piece]
-            dest = rounded[name][t0 // 2][:].rearrange("p (t g i j) -> p t g j i", t=2, i=4, j=PACK)[:, t0 % 2 : t0 % 2 + t1 - t0, g0:g1]
-            copy(dest, raw[name][piece][:].rearrange("p j (g t i) -> p t g j i", t=4, i=4)[:, t0:t1])
+            dest = rounded[name][u][:].rearrange(f"p (t g i j) -> {order}", t=2, i=2, j=PACK)[:, 2 * g0 : 2 * g1]
+            rows = raw[name][piece][:].rearrange(f"p j (g t i) -> {order}", t=4, i=2)[:, :, 2 * u : 2 * u + 2]
+            return dest, rows
 
-        def round_tiles_gpsimd(name, piece, t0, t1):
-            g0, g1 = GROUPS[name][piece]
-            dest = rounded[name][t0 // 2][:].rearrange("p (t g i j) -> p g t i j", t=2, i=4, j=PACK)[:, g0:g1, t0 % 2 : t0 % 2 + t1 - t0]
-            nc.gpsimd.tensor_scalar(dest, raw[name][piece][:].rearrange("p j (g t i) -> p g t i j", t=4, i=4)[:, :, t0:t1], 1.0, 0.0, ALU.mult, ALU.add)
+        def round_pair(name, piece, u, copy):
+            copy(*round_views(name, piece, u, "p g t j i"))
+
+        def round_gpsimd(dest, rows):
+            nc.gpsimd.tensor_scalar(dest, rows, 1.0, 0.0, ALU.mult, ALU.add)
 
         def quantize_weights(name, u):
             cols = slice(u * HALF, (u + 1) * HALF)
@@ -160,18 +162,18 @@ def tile_picked_zlink_reluxsoft_p_kernel(tc, x_words, x_scales, w1, w2, offs, ds
 
         xd_scales = gather_scales("xd_scales", dst_list[:])
         xs_scales = gather_scales("xs_scales", src_list[:])
-        first_dest = rounded["w2"][0][:].rearrange("p (t g i j) -> p t g j i", t=2, i=4, j=PACK)
-        first_rows = raw["w2"][0][:].rearrange("p j (g t i) -> p t g j i", t=4, i=4)
-        nc.scalar.copy(first_dest[:, 0, 0, 0:1], first_rows[:, 0, 0, 0:1])
-        nc.scalar.copy(first_dest[:, 0, 0, 1:PACK], first_rows[:, 0, 0, 1:PACK])
-        nc.scalar.copy(first_dest[:, 0, 1:], first_rows[:, 0, 1:])
-        nc.scalar.copy(first_dest[:, 1], first_rows[:, 1])
-        second_rows = raw["w2"][0][:].rearrange("p j (g t i) -> p g t i j", t=4, i=4)[:, 0:24, 2:4]
-        nc.gpsimd.tensor_scalar(rounded["w2"][1][:].rearrange("p (t g i j) -> p g t i j", t=2, i=4, j=PACK)[:, 0:24], second_rows, 1.0, 0.0, ALU.mult, ALU.add)
-        nc.scalar.copy(rounded["w2"][1][:].rearrange("p (t g i j) -> p t g j i", t=2, i=4, j=PACK)[:, :, 24:32], first_rows[:, 2:4, 24:32])
+        dest, rows = round_views("w2", 0, 0, "p g t j i")
+        nc.scalar.copy(dest[:, 0:2, :, 0], rows[:, 0:2, :, 0])
+        nc.scalar.copy(dest[:, 0:2, :, 1:PACK], rows[:, 0:2, :, 1:PACK])
+        nc.scalar.copy(dest[:, 2:], rows[:, 2:])
+        dest, rows = round_views("w2", 0, 1, "p g t i j")
+        round_gpsimd(dest[:, 0:48], rows[:, 0:48])
+        dest, rows = round_views("w2", 0, 1, "p g t j i")
+        nc.scalar.copy(dest[:, 48:64], rows[:, 48:64])
         xd_first = gather_words("xd_first", dst_list[:, 0:8])
         quantize_weights("w2", 0)
-        quantize_weights("w2", 1)
+        for t in (2, 3):
+            nc.vector.quantize_mx(out=chunk(w_words["w2"], t).bitcast(FP8X4), scales=chunk(w_scales["w2"], t), in_=rounded["w2"][1][:, (t - 2) * H : (t - 1) * H])
         xd_second = gather_words("xd_second", dst_list[:, 8:16], 16384 + 2048)
         xd_rest = gather_words("xd_rest", dst_list[:, 16:32], 16384)
         xd_words = [xd_first[:], xd_second[:], chunk(xd_rest, 0), chunk(xd_rest, 1)]
@@ -179,11 +181,11 @@ def tile_picked_zlink_reluxsoft_p_kernel(tc, x_words, x_scales, w1, w2, offs, ds
         d_banks = [psum.tile([P, PACK, CHUNK], F32, name=f"d_bank{c}", tag="bank") for c in range(CHUNKS)]
         for c in range(CHUNKS):
             hidden_matmuls(d_banks[c], "w2", xd_words[c], chunk(xd_scales, c), 0, PACK)
-        round_tiles("w1", 0, nc.scalar.copy, 0, 2)
-        round_tiles_gpsimd("w1", 0, 2, 4)
+        round_pair("w1", 0, 0, nc.scalar.copy)
+        round_gpsimd(*round_views("w1", 0, 1, "p g t i j"))
         relu(d_part(0), d_banks[0])
-        round_tiles("w1", 1, nc.vector.tensor_copy, 0, 2)
-        round_tiles("w1", 1, nc.vector.tensor_copy, 2, 4)
+        round_pair("w1", 1, 0, nc.vector.tensor_copy)
+        round_pair("w1", 1, 1, nc.vector.tensor_copy)
         quantize_weights("w1", 0)
         quantize_weights("w1", 1)
         xs_second = gather_words("xs_second", src_list[:, 8:16], 24576 + 256 * 16)

from contextlib import ExitStack

import concourse.mybir as mybir

K, T, S, V, H = 512, 1024, 512, 512, 512
FLOPS = 2 * K * H * S + 2 * K * H * V + 2 * H * S * V

F32 = mybir.dt.float32
BF16 = mybir.dt.bfloat16
I32 = mybir.dt.int32
U32 = mybir.dt.uint32
U16 = mybir.dt.uint16
U8 = mybir.dt.uint8
FP8X4 = mybir.dt.float8_e4m3fn_x4
ACT = mybir.ActivationFunctionType
ALU = mybir.AluOpType

P = 128
PACK = 4
CHUNK = 128
CHUNKS = 4
HALF = 256
GROUPS = {"w2": [(0, 32)], "w1": [(0, 16), (16, 32)]}


def tile_picked_zlink_reluxsoft_p_kernel(tc, x_words, x_scales, w1, w2, offs, dst, out):
    nc = tc.nc
    with ExitStack() as ctx:
        keep = ctx.enter_context(tc.tile_pool(name="keep", bufs=1))
        shared = ctx.enter_context(tc.tile_pool(name="shared", bufs=1))
        psum = ctx.enter_context(tc.psum_pool(name="psum", bufs=8))

        dst_list = keep.tile([P, V // 16], U16, name="dst_list")
        src_list = keep.tile([P, S // 16], U16, name="src_list")
        scale_table = keep.tile([P, T], U8, name="scale_table", align_bytes=256)
        word_table = keep.tile([P, T], I32, name="word_table", align_bytes=256)
        raw = {
            "w2": [shared.tile([P, PACK, H], F32, name="raw_w2", align_bytes=256, offset=16384)],
            "w1": [shared.tile([P, PACK, 16 * (g1 - g0)], F32, name=f"raw_w1_{g0}", align_bytes=256, offset=24576 + 256 * g0) for g0, g1 in GROUPS["w1"]],
        }

        def load_scales(q, queue):
            queue.dma_start(scale_table[32 * q : 32 * q + 4, :].bitcast(I32), x_scales[0, 4 * q : 4 * q + 4, :].bitcast(I32))

        def gather_scales(name, offsets):
            scales = keep.tile([P, 16 * offsets.shape[1]], U8, name=name, align_bytes=256)
            nc.vector.tensor_copy(scales[:], scale_table[:].indirect(offsets))
            return scales

        def gather_words(name, offsets, at=None):
            words = (keep if at is None else shared).tile([P, 16 * offsets.shape[1]], U32, name=name, align_bytes=256, offset=at)
            nc.vector.tensor_copy(words[:], word_table[:].bitcast(U32).indirect(offsets))
            return words

        rounded = {
            n: [shared.tile([P, HALF * PACK], BF16, name=f"rounded_{n}_{u}", align_bytes=256, offset=at + 2048 * u) for u in range(2)]
            for n, at in (("w2", 0), ("w1", 4096))
        }
        w_words = {n: keep.tile([P, H], U32, name=f"words_{n}", align_bytes=256) for n in ("w1", "w2")}
        w_scales = {n: keep.tile([P, H], U8, name=f"scales_{n}", align_bytes=256) for n in ("w1", "w2")}

        def round_views(name, piece, u, order):
            g0, g1 = GROUPS[name][piece]
            dest = rounded[name][u][:].rearrange(f"p (t g i j) -> {order}", t=2, i=2, j=PACK)[:, 2 * g0 : 2 * g1]
            rows = raw[name][piece][:].rearrange(f"p j (g t i) -> {order}", t=4, i=2)[:, :, 2 * u : 2 * u + 2]
            return dest, rows

        def round_pair(name, piece, u, copy):
            copy(*round_views(name, piece, u, "p g t j i"))

        def round_gpsimd(dest, rows):
            nc.gpsimd.tensor_scalar(dest, rows, 1.0, 0.0, ALU.mult, ALU.add)

        def quantize_weights(name, u):
            cols = slice(u * HALF, (u + 1) * HALF)
            nc.vector.quantize_mx(out=w_words[name][:, cols].bitcast(FP8X4), scales=w_scales[name][:, cols], in_=rounded[name][u][:])

        def hidden_matmuls(bank, name, words, scales, t0, t1):
            for t in range(t0, t1):
                cols = slice(t * P, (t + 1) * P)
                nc.tensor.matmul_mx(
                    out=bank[:, t, :],
                    lhsT=w_words[name][:, cols].bitcast(FP8X4),
                    lhsT_scale=w_scales[name][:, cols],
                    rhs=words.bitcast(FP8X4),
                    rhs_scale=scales,
                    start=True,
                    stop=True,
                )

        def relu(hidden, bank):
            nc.scalar.activation(hidden.rearrange("p (n t) -> p n t", t=PACK), bank[:].rearrange("p t n -> p n t"), ACT.Relu)

        def chunk(tile, c):
            return tile[:, c * CHUNK : (c + 1) * CHUNK]

        d_words = keep.tile([P, V], U32, name="d_words", align_bytes=256)
        d_scales = keep.tile([P, V], U8, name="d_scales", align_bytes=256)
        d_hidden = keep.tile([P, V * PACK], BF16, name="d_hidden", align_bytes=256)
        p_hidden = [keep.tile([P, CHUNK * PACK], BF16, name=f"p_hidden{c}", align_bytes=256) for c in range(CHUNKS)]
        p_words = [keep.tile([P, CHUNK], U32, name=f"p_words{c}", align_bytes=256) for c in range(CHUNKS)]
        p_scales = [keep.tile([P, CHUNK], U8, name=f"p_scales{c}", align_bytes=256) for c in range(CHUNKS)]

        def d_part(c):
            return d_hidden[:, c * CHUNK * PACK : (c + 1) * CHUNK * PACK]

        def quantize_p(c):
            nc.vector.quantize_mx(out=p_words[c][:].bitcast(FP8X4), scales=p_scales[c][:], in_=p_hidden[c][:])

        neg_max = {}
        total = {c: keep.tile([P, 1], F32, name=f"total{c}") for c in range(CHUNKS)}
        inverse = [keep.tile([P, 1], F32, name=f"inverse{c}") for c in range(CHUNKS)]
        powers = [keep.tile([P, V], F32, name=f"powers{c}", align_bytes=256) for c in range(CHUNKS)]
        result = [keep.tile([P, V], F32, name=f"result{c}", align_bytes=256) for c in range(CHUNKS)]

        def score_matmul(c):
            score = psum.tile([P, V], F32, name="score", tag="bank")
            nc.tensor.matmul_mx(
                out=score[:],
                lhsT=p_words[c][:].bitcast(FP8X4),
                lhsT_scale=p_scales[c][:],
                rhs=d_words[:].bitcast(FP8X4),
                rhs_scale=d_scales[:],
                start=True,
                stop=True,
            )
            return score

        def row_max(c, score):
            nc.vector.tensor_reduce(neg_max[c][:], score[:], mybir.AxisListType.X, ALU.max, negate=True)

        def exponentials(c, score):
            nc.scalar.activation(powers[c][:], score[:], ACT.Exp, bias=neg_max[c][:], accum_out=total[c][:])

        def invert(c):
            nc.vector.reciprocal(inverse[c][:], total[c][:])

        def normalise_gpsimd(c):
            nc.gpsimd.tensor_scalar(result[c][:], powers[c][:], inverse[c][:], 0.0, ALU.mult, ALU.add)

        def normalise_vector(c):
            nc.vector.tensor_scalar(result[c][:], powers[c][:], inverse[c][:], None, ALU.mult)

        def store(c):
            nc.sync.dma_start(out[c * CHUNK : (c + 1) * CHUNK, :], result[c][:])

        nc.vector.memset(scale_table[:].bitcast(I32), 0)
        w1_rows = w1.rearrange("(p j) c -> p j c", j=PACK)
        w2_flat = raw["w2"][0][:].rearrange("p j c -> p (j c)")
        w2_runs = w2.rearrange("(p j) c -> p (j c)", j=PACK)
        nc.sync.dma_start(dst_list[:], dst)
        nc.sync.dma_start(w2_flat[:, 0:640], w2_runs[:, 0:640])
        nc.sync.dma_start(src_list[:], offs)
        load_scales(0, nc.sync)
        load_scales(1, nc.sync)
        load_scales(2, nc.scalar)
        load_scales(3, nc.scalar)
        nc.sync.dma_start(w2_flat[:, 640:], w2_runs[:, 640:])
        nc.sync.dma_start(word_table[:], x_words[0].rearrange("p c r -> p (c r)").bitcast(I32))
        for h, (g0, g1) in enumerate(GROUPS["w1"]):
            nc.sync.dma_start(raw["w1"][h][:], w1_rows[:, :, 16 * g0 : 16 * g1])

        xd_scales = gather_scales("xd_scales", dst_list[:])
        xs_scales = gather_scales("xs_scales", src_list[:])
        dest, rows = round_views("w2", 0, 0, "p g t j i")
        nc.scalar.copy(dest[:, 0:2, :, 0], rows[:, 0:2, :, 0])
        nc.scalar.copy(dest[:, 0:2, :, 1:PACK], rows[:, 0:2, :, 1:PACK])
        nc.scalar.copy(dest[:, 2:], rows[:, 2:])
        dest, rows = round_views("w2", 0, 1, "p g t i j")
        round_gpsimd(dest[:, 0:48], rows[:, 0:48])
        dest, rows = round_views("w2", 0, 1, "p g t j i")
        nc.scalar.copy(dest[:, 48:64], rows[:, 48:64])
        xd_first = gather_words("xd_first", dst_list[:, 0:8])
        quantize_weights("w2", 0)
        for t in (2, 3):
            nc.vector.quantize_mx(out=chunk(w_words["w2"], t).bitcast(FP8X4), scales=chunk(w_scales["w2"], t), in_=rounded["w2"][1][:, (t - 2) * H : (t - 1) * H])
        xd_second = gather_words("xd_second", dst_list[:, 8:16], 16384 + 2048)
        xd_rest = gather_words("xd_rest", dst_list[:, 16:32], 16384)
        xd_words = [xd_first[:], xd_second[:], chunk(xd_rest, 0), chunk(xd_rest, 1)]
        xs_first = gather_words("xs_first", src_list[:, 0:8], 16384 + 1024)
        d_banks = [psum.tile([P, PACK, CHUNK], F32, name=f"d_bank{c}", tag="bank") for c in range(CHUNKS)]
        for c in range(CHUNKS):
            hidden_matmuls(d_banks[c], "w2", xd_words[c], chunk(xd_scales, c), 0, PACK)
        round_pair("w1", 0, 0, nc.scalar.copy)
        round_gpsimd(*round_views("w1", 0, 1, "p g t i j"))
        relu(d_part(0), d_banks[0])
        round_pair("w1", 1, 0, nc.vector.tensor_copy)
        round_pair("w1", 1, 1, nc.vector.tensor_copy)
        quantize_weights("w1", 0)
        quantize_weights("w1", 1)
        xs_second = gather_words("xs_second", src_list[:, 8:16], 24576 + 256 * 16)
        xs_rest = gather_words("xs_rest", src_list[:, 16:32], 24576 + 256 * 16 + 512)
        xs_words = [xs_first[:], xs_second[:], chunk(xs_rest, 0), chunk(xs_rest, 1)]
        for c in range(1, CHUNKS):
            relu(d_part(c), d_banks[c])
        nc.vector.quantize_mx(out=d_words[:].bitcast(FP8X4), scales=d_scales[:], in_=d_hidden[:])
        for c in range(CHUNKS):
            bank = psum.tile([P, PACK, CHUNK], F32, name="p_bank", tag="bank")
            hidden_matmuls(bank, "w1", xs_words[c], chunk(xs_scales, c), 0, PACK)
            relu(p_hidden[c][:], bank)
            quantize_p(c)
        for c in range(CHUNKS):
            neg_max[c] = shared.tile([P, 1], F32, name=f"neg_max{c}", offset=8192 + 32 * (c % 2))
            score = score_matmul(c)
            row_max(c, score)
            exponentials(c, score)
            invert(c)
            if c < 1:
                normalise_gpsimd(c)
                store(c)
        for c in range(1, CHUNKS - 1):
            normalise_vector(c)
            store(c)
        c = CHUNKS - 1
        for h in range(2):
            cols = slice(h * HALF, (h + 1) * HALF)
            nc.vector.tensor_scalar(result[c][:, cols], powers[c][:, cols], inverse[c][:], None, ALU.mult)
            nc.sync.dma_start(out[c * CHUNK : (c + 1) * CHUNK, cols], result[c][:, cols])
